import numpy as np, ml_dtypes
CORES = [40,64,80,88,96,104,120,144]
N = 8
BF = ml_dtypes.bfloat16
P, S, M, RO = 512, 2, 4, 5
W, E, Q = N * P, P // S, 2 ** M
def pack(nm, mk):
    z = (nm << M) | mk
    return {"kin": np.ascontiguousarray(z.reshape(128, N, P).transpose(1, 0, 2)).astype(np.int32)}
def town(rng, caps, nin, skew=False):
    order = rng.permutation(W); pos = np.empty(W, np.int64); pos[order] = np.arange(W); blk = pos >> 6; nb = W >> 6
    if skew: key = rng.standard_exponential((8, W, 64), dtype=np.float32) * np.exp2(np.arange(64) * 0.125).astype(np.float32)
    else: key = rng.random((8, W, 64), dtype=np.float32) + 2 * (np.arange(64) >= rng.choice(np.array(caps), nb)[blk][:, None]).astype(np.float32)
    inn = order[64 * blk[None, :, None] + np.argsort(key, axis=-1)[..., :16]]
    ob = (blk + 1 + rng.integers(0, nb - 1, (8, W))) % nb
    far = (rng.integers(0, 64, (8, W, 1)) + (2 * rng.integers(0, 32, (8, W, 1)) + 1) * np.arange(16)) & 63
    m = np.argsort(rng.random((8, W, 16)), axis=-1) < rng.choice(np.array(nin), nb)[blk][None, :, None]
    return np.ascontiguousarray(np.where(m, inn, order[64 * ob[..., None] + far]).transpose(0, 2, 1))
def flips(rng, q):
    f = np.zeros((8, 16, W), np.int64)
    for m in range(M): f |= (rng.random((8, 16, W), dtype=np.float32) < q).astype(np.int64) << m
    return f
def marks(rng, nm, shares):
    lab = rng.integers(0, Q, W)
    return lab[None, None, :] ^ lab[nm] ^ flips(rng, rng.choice(np.array(shares), (8, 1, W)))
def setup_inputs(rng):
    nm = town(rng, [20, 32, 48, 64], [8, 10, 12, 14, 15])
    return pack(nm, marks(rng, nm, [0.05, 0.2, 0.5]))
def setup_inputs_spread(rng):
    nm = town(rng, [64], [9, 12, 14], True); k = np.argsort(rng.random((8, 16, W)), axis=1)
    wide_ = (rng.integers(0, W, (8, 1, W)) + k * rng.integers(1, W // 16, (8, 1, W))) % W
    nm = np.where(rng.random((8, 1, W)) < 0.33, wide_, nm)
    return pack(nm, flips(rng, rng.choice(np.array([0.02, 0.1, 0.5, 0.9, 0.98]), (8, 1, W))))
def setup_inputs_ends(rng):
    e = np.concatenate([np.arange(8), np.arange(W - 8, W)]); x = np.array([8, 9, W - 10, W - 9]); pool = np.concatenate([e, x])
    full = rng.random(W) < 0.5; kind = rng.integers(0, 6, W)
    for r in range(N): kind[P * r + P - 22:P * r + P] = (np.arange(22) + r) % 6
    full[e] = True; full[x] = False; kind[e] = 0; kind[x] = 4
    idx = np.where(full[None, :, None], np.argsort(rng.random((8, W, 16)), axis=-1), np.argsort(rng.random((8, W, 20)), axis=-1)[..., :16])
    nm = np.ascontiguousarray(pool[idx].transpose(0, 2, 1))
    lab = rng.integers(0, 2, W); lab[0] = 0; lab[W - 1] = 1
    half = np.broadcast_to((np.argsort(rng.random((8, W)), axis=0) < 4)[:, None, :], (8, 16, W))
    spot = np.arange(128).reshape(8, 16, 1) == np.where(rng.random(W) < 0.5, 127, rng.integers(0, 128, W))[None, None, :]
    f = np.zeros((8, 16, W), bool)
    for c, v in ((1, half), (2, half & ~spot), (3, half | spot), (4, rng.random((8, 16, W)) < 0.5), (5, ~spot)): f = np.where(kind == c, v, f)
    return pack(nm, (lab[None, None, :] ^ lab[nm] ^ f.astype(np.int64)) * (Q - 1))
def setup_inputs_crowd(rng):
    rot = rng.permutation(N)
    order = np.ascontiguousarray((np.argsort(rng.random((N, P)), axis=1) + P * rot[:, None]).reshape(N, P >> 4, 16).transpose(1, 0, 2)).reshape(-1)
    pos = np.empty(W, np.int64); pos[order] = np.arange(W); blk = pos // (16 * N); lay = (pos >> 4) % N; nb = P >> 4
    typ = (rng.permutation(nb) % 3)[blk]
    p = (16 * N * blk + 16 * np.where(typ == 2, 0, (lay + 1) % N))[None, :, None] + np.argsort(rng.random((8, W, 16)), axis=-1)
    gs = rng.integers(0, 8, (nb, N))[blk, lay]; js = rng.integers(0, 16, (nb, N))[blk, lay]
    hit = (typ == 1)[None, :] & (np.arange(8)[:, None] == gs[None, :]) & ((pos & 15) == js)[None, :]
    nm = np.ascontiguousarray(order[np.where(hit[..., None], (p + 16 * N) % W, p)].transpose(0, 2, 1))
    pat = np.argsort(rng.random((nb, 8, M)), axis=1) < rng.choice(np.array([0, 3, 4, 5, 8]), (nb, 1, M))
    u = np.sum(pat.astype(np.int64) << np.arange(M), axis=2)[blk].T
    on = np.where(typ == 2, lay > 0, (lay & 1) == 0)
    noise = np.where(rng.random((8, 16, W)) < (rng.choice(np.array([0.0, 0.04]), nb)[blk])[None, None, :], rng.integers(0, Q, (8, 16, W)), 0)
    return pack(nm, np.where(on[None, :], u, 0)[:, None, :] ^ noise)
def put(a, k, v, on):
    w = a[k].copy(); a[:] = np.where((a == v) & on, w, a); a[k] = np.where(on, v, a[k])
def setup_inputs_corners(rng):
    nm = town(rng, [20, 40, 64], [10, 13]); p = np.arange(W); every = np.ones(W, bool)
    nm[7] = (p + 1 + np.argsort(rng.random((16, W)), axis=0)) % W
    nm[6] = (p + W - 8 + np.argsort(rng.random((16, W)), axis=0)) % W
    put(nm[0], 0, p, every)
    on = ((p >> 5) & 1) == rng.integers(0, 2)
    put(nm[1], 1, (p + 1) % W, on); put(nm[1], 4, (p + W - 1) % W, on)
    put(nm[2], 2, np.where(rng.random(W) < 0.5, 0, W - 1), every)
    put(nm[2], 5, np.where(p == 0, W - 1, 0), (p == 0) | (p == W - 1))
    put(nm[3], 3, (p + 1) % W, every); put(nm[3], 6, (p + 2) % W, every)
    put(nm[4], 15, np.zeros(W, np.int64), every); put(nm[5], 15, np.full(W, W - 1), every); put(nm[5], 0, np.zeros(W, np.int64), rng.random(W) < 0.5)
    kind = rng.integers(0, 4, (8, W >> 5))[:, p >> 5][:, None, :]
    mk = marks(rng, nm, [0.0, 0.1]); rnd = rng.integers(0, Q, (8, 16, W))
    return pack(nm, np.where(kind == 0, 0, np.where(kind == 1, Q - 1, np.where(kind == 2, mk, rnd))))
def setup_inputs_calm(rng):
    nm = town(rng, [64], [2, 3, 4, 5, 6]); p = np.arange(W); i = rng.permutation(E - 1)[:9]
    one = np.add.outer(P * np.arange(N), S * i[:8]).reshape(-1); two = one + 1
    h = P * int(rng.integers(0, N)) + S * int(i[8])
    on1 = np.zeros(W, bool); on1[one] = True
    on2 = np.zeros(W, bool); on2[two] = True
    for g in range(8):
        put(nm[g], 15, W - 1, on1)
        for j in range(8): put(nm[g], 4 + j, P * ((p // P + 1) % N) + S * int(i[j]), on2)
    put(nm[0], 0, h, on1); put(nm[S], S, h, on1); put(nm[1], 1, h, on2)
    put(nm[0], 0, h + 1, p == h); put(nm[0], 3, W - 1, p == h); put(nm[1], 4, W - 1, p == h); put(nm[S], S + 3, W - 1, p == h)
    put(nm[0], 3, h, p == h + 1)
    mk = marks(rng, nm, [0.1, 0.5])
    mk[:, 15, one] = np.where(np.argsort(rng.random((8, 8 * N)), axis=0) < 2, 0, Q - 1)
    mk[0, 0, one] = Q - 1; mk[S, S, one] = Q - 1; mk[:, 4:12, two] = 0
    mk[0, 3, h] = 0; mk[1, 4, h] = 0; mk[S, S + 3, h] = 0
    return pack(nm, mk)
def check_inputs(d):
    bad = []; z = np.asarray(d["kin"]).astype(np.int64)
    if np.min(z) < 0 or np.max(z) > Q * W - 1: bad.append("range of kin")
    s = np.sort((z >> M).reshape(N, 8, 16, P), axis=2)
    if np.any(s[:, :, 1:] == s[:, :, :-1]): bad.append("equal names in one list of kin")
    return bad
def reference(kin):
    z = np.ascontiguousarray(kin.astype(np.int64).transpose(1, 0, 2)).reshape(8, 16, W)
    for t in range(RO):
        a = np.add.outer(P * np.arange(N), S * np.arange(E) + t % S).reshape(-1)
        nm = z >> M; mk = z & (Q - 1)
        c = nm[t, t, a]; b = nm[t, t + 3, c]
        tes = np.zeros((8, 16, N * E), bool); own = np.zeros((8, 16, N * E), bool); val = np.zeros((8, 16, N * E), np.int64)
        for g in range(8):
            ca = nm[g][:, a]; ma = mk[g][:, a]
            eq = nm[g][:, ca] == b
            m2 = np.add.reduce(np.where(eq, mk[g][:, ca], 0), axis=0)
            own[g] = ca == b; tes[g] = np.any(eq, axis=0) | own[g]
            val[g] = np.where(own[g], ma, ma ^ m2)
        n = np.sum(tes.astype(np.int64), axis=(0, 1)); won = np.zeros(N * E, np.int64); dif = np.zeros((8, 16, N * E), np.int64)
        for m in range(M):
            bit = (val >> m) & 1
            w = (2 * np.sum(np.where(tes, bit, 0), axis=(0, 1)) > n).astype(np.int64)
            won = won + (w << m); dif = dif + (bit != w)
        key = np.where(own, 1000, np.where(tes, dif, -1))
        row = np.argmax(key, axis=1)
        gi, ai = np.nonzero(np.any(tes, axis=1) & (b != a))
        z[gi, row[gi, ai], a[ai]] = (Q * b + won)[ai]
    return {"yk": np.ascontiguousarray(z.reshape(128, N, P).transpose(1, 0, 2)).astype(np.float32)}

@@ -1,0 +1,514 @@
+import math
+from concourse.bass import DstId, RemoteDMATransfer
+from concourse.mybir import AluOpType as A, ActivationFunctionType as F
+
+N, P, E, RO = 8, 512, 256, 5
+MAGIC = 201326592.0
+LN64 = math.log(64.0)
+IDS = [-1.0, 2.0, 40.0, -4.5, -60.0, -5120.0]
+
+SCRATCH = {
+    "kin_i": ("sbuf", [128, P], "int32"),
+    "msg0": ("sbuf", [128, P], "uint16"),
+    "land0": ("sbuf", [128, N * P], "uint16"),
+    "tab": ("sbuf", [128, N * P], "float32"),
+    "gat": ("sbuf", [128, 16 * E], "float32"),
+    "dif": ("sbuf", [128, 16 * E], "bfloat16"),
+    "off": ("sbuf", [128, E], "uint16"),
+    "ui": ("sbuf", [128, E], "int32"),
+    "tmpi": ("sbuf", [128, 6 * E], "int32"),
+    "n16": ("sbuf", [128, E], "int32"),
+    "ma": ("sbuf", [128, E], "bfloat16"),
+    "e16": ("sbuf", [128, E], "float32"),
+    "eabs": ("sbuf", [128, E], "float32"),
+    "nown": ("sbuf", [128, E], "bfloat16"),
+    "mul": ("sbuf", [128, E], "float32"),
+    "skip": ("sbuf", [128, E], "bfloat16"),
+    "pi": ("sbuf", [128, E], "int32"),
+    "uu": ("sbuf", [128, 4 * E], "int32"),
+    "tes": ("sbuf", [128, E], "bfloat16"),
+    "zz": ("sbuf", [128, 4 * E], "bfloat16"),
+    "gg": ("sbuf", [128, 4 * E], "bfloat16"),
+    "om": ("sbuf", [128, E], "bfloat16"),
+    "xx": ("sbuf", [128, E], "bfloat16"),
+    "win": ("sbuf", [128, E], "bfloat16"),
+    "ss": ("sbuf", [128, E], "float32"),
+    "yo": ("sbuf", [128, P], "float32"),
+    "a16": ("sbuf", [128, P], "float32"),
+    "one": ("sbuf", [128, 128], "float32"),
+    "id32": ("sbuf", [128, 128], "float32"),
+    "ids": ("sbuf", [128, 128 * len(IDS)], "bfloat16"),
+    "sel": ("sbuf", [128, 128 * RO], "float32"),
+    "rp": ("sbuf", [128, 144], "bfloat16"),
+    "lraw": ("sbuf", [128, 128], "float32"),
+    "tri": ("sbuf", [128, 128], "bfloat16"),
+    "vn": ("sbuf", [128, 128], "bfloat16"),
+    "vz": ("sbuf", [128, 128], "bfloat16"),
+    "wm": ("sbuf", [128, 128], "bfloat16"),
+}
+for _t in range(1, RO):
+    SCRATCH["msg%d" % _t] = ("sbuf", [128, E], "uint16")
+    SCRATCH["land%d" % _t] = ("sbuf", [128, N * E], "uint16")
+for _b in "abcdefgh":
+    SCRATCH["ps" + _b] = ("psum", [128, 512], "float32")
+
+SEMAPHORES = (["sv", "ss", "sp", "sg", "loaded", "stored", "sent"] + ["rin%d" % t for t in range(RO)]
+              + ["arr%d_%d" % (t, r) for t in range(RO) for r in range(N)])
+
+
+def bits(engs):
+    m = 0
+    for e in engs:
+        m |= 1 << e
+    return m
+
+
+def routes(T, topo):
+    cores = list(T.cores)
+    out = []
+    for r, c in enumerate(cores):
+        near = [s for s in range(N) if s != r and topo.may_write(c, cores[s])]
+        far = [s for s in range(N) if s != r and s not in near]
+        able = [h for h in topo.cores_of(c) if h != c and all(topo.may_write(h, cores[s]) for s in far)]
+        able.sort(key=lambda h: topo.die(h) == topo.die(c))
+        i = sorted(near + [r]).index(r)
+        far = far[i % len(far):] + far[:i % len(far)]
+        near = [s for s in near if s > r] + [s for s in near if s < r]
+        out.append((near, {able[0]: far[0::2], able[1]: far[1::2]}))
+    return out
+
+
+def one_to_many(g, T, topo, src_core, dst_cores, src, dst, sem, engs):
+    ids = []
+    for d in dst_cores:
+        rid, pid = topo.addr(d, src_core)
+        ids.append(DstId(rid=rid, pnc=pid))
+    return RemoteDMATransfer(dst_ids=ids, dma_engine_mask=bits(engs), remote_sem=sem, srcs=[src], dsts=[dst] * len(ids))
+
+
+def width(x):
+    return P if x == 0 else E
+
+
+def helper_program(g, core, T, topo, r, dsts):
+    cores = list(T.cores)
+    n_in = len(topo.engines(cores[r], core)) // 2
+    engs = topo.engines(core, cores[dsts[0]])
+    for x in range(RO):
+        w = width(x)
+        g.wait_ge(T.sem["rin%d" % x], n_in)
+        tr = one_to_many(g, T, topo, core, [cores[s] for s in dsts], T["msg%d" % x][:, :],
+                         T["land%d" % x][:, r * w:(r + 1) * w], T.sem["arr%d_%d" % (x, r)], engs)
+        g.remote_dma_fused([tr], local_sem=T.sem.sent)
+    g.wait_ge(T.sem.sent, RO * len(engs))
+
+
+def emit(g, T, ops):
+    q = {"v": g.vector, "s": g.scalar, "p": g.tensor, "g": g, "y": g.sync}
+    semname = {"v": "sv", "s": "ss", "p": "sp", "g": "sg"}
+    lastw, readers, bank = {}, {}, {}
+    deps = []
+    for i, (e, fn, rd, wr, bk, ev) in enumerate(ops):
+        d = set()
+        for k in rd:
+            if k in lastw:
+                d.add(lastw[k])
+        for k in wr:
+            if k in lastw:
+                d.add(lastw[k])
+            d.update(readers.get(k, []))
+        for k in bk:
+            for e2, j in bank.get(k, {}).items():
+                if e2 != e:
+                    d.add(j)
+        d.discard(i)
+        if e == "p":
+            d = set(j for j in d if ops[j][0] != "p")
+        best = {}
+        keep = set()
+        for j in d:
+            if ops[j][5] is not None:
+                keep.add(j)
+            else:
+                best[ops[j][0]] = max(best.get(ops[j][0], -1), j)
+        keep.update(best.values())
+        deps.append(keep)
+        for k in rd:
+            readers.setdefault(k, []).append(i)
+        for k in wr:
+            lastw[k] = i
+            readers[k] = []
+        for k in bk:
+            bank.setdefault(k, {})[e] = i
+    seen = {}
+    for i, op in enumerate(ops):
+        keep = set()
+        for j in deps[i]:
+            if ops[j][5] is not None:
+                key, val = (op[0], ops[j][5][0]), ops[j][5][1]
+            else:
+                key, val = (op[0], ops[j][0]), j
+            if seen.get(key, -1) < val:
+                seen[key] = val
+                keep.add(j)
+        deps[i] = keep
+    need = set()
+    for d in deps:
+        need.update(d)
+    count = {"v": 0, "s": 0, "p": 0, "g": 0}
+    event = {}
+    for i, (e, fn, rd, wr, bk, ev) in enumerate(ops):
+        for j in sorted(deps[i]):
+            q[e].wait_ge(T.sem[event[j][0]], event[j][1])
+        ins = fn() if fn is not None else None
+        if ev is not None:
+            event[i] = ev
+        elif i in need:
+            count[e] += 1
+            ins.then_inc(T.sem[semname[e]], 1)
+            event[i] = (semname[e], count[e])
+
+
+def rank_program(g, core, T, topo):
+    cores = list(T.cores)
+    plan = routes(T, topo)
+    r = T.rank_of(core)
+    if r is None:
+        for s in range(N):
+            if core in plan[s][1]:
+                helper_program(g, core, T, topo, s, plan[s][1][core])
+        return
+    near, helpers = plan[r]
+    from_near = sorted(near, key=lambda s: plan[s][0].index(r))
+    from_far = sorted([s for s in range(N) if s != r and s not in near],
+                      key=lambda s: [d.index(r) for d in plan[s][1].values() if r in d][0])
+    senders = from_near + from_far
+    hs = list(helpers.keys())
+    V, S, PE = g.vector, g.scalar, g.tensor
+    ops = []
+
+    def op(e, fn, rd=(), wr=(), bk=(), ev=None):
+        ops.append((e, fn, list(rd), list(wr), list(bk), ev))
+
+    def ts(out, in0, s1, s2, o0, o1, rd, wr, bk=()):
+        if o1 is None:
+            op("v", lambda: V.tensor_scalar(out, in0, s1, None, o0), rd, wr, bk)
+        else:
+            op("v", lambda: V.tensor_scalar(out, in0, s1, s2, o0, o1), rd, wr, bk)
+
+    def tt(out, in0, in1, o, rd, wr, bk=()):
+        op("v", lambda: V.tensor_tensor(out, in0, in1, o), rd, wr, bk)
+
+    def cp(out, in_, rd, wr, bk=()):
+        op("v", lambda: V.tensor_copy(out, in_), rd, wr, bk)
+
+    def ms(ap, val, wr):
+        op("v", lambda: V.memset(ap, val), (), wr)
+
+    def act(out, in_, f, bias, scale, rd, wr, bk=()):
+        op("s", lambda: S.activation(out, in_, f, bias=bias, scale=scale), rd, wr, bk)
+
+    def mm(out, lhsT, rhs, st, sp, rd, wr, bk):
+        op("p", lambda: PE.matmul(out, lhsT, rhs, st, sp), rd, wr, bk)
+
+    def asel(ap, pat, cmp, fill, base, cm, tok, src=None, srctok=None):
+        op("g", lambda: g.affine_select(ap, ap if src is None else src, pat, cmp, fill, base, cm),
+           [tok if srctok is None else srctok], [tok])
+
+    def ident(x):
+        i = IDS.index(x)
+        return T.ids[:, 128 * i:128 * (i + 1)]
+
+    sent = [0]
+
+    def send(x):
+        w = width(x)
+        src = T["msg%d" % x][:, :]
+        on = topo.engines(core, hs[0])
+        h = len(on) // 2
+        trs = [one_to_many(g, T, topo, core, [hs[i]], src, src, T.sem["rin%d" % x], on[i * h:(i + 1) * h]) for i in range(2)]
+        offc = topo.engines(core, cores[near[0]])
+        tr = one_to_many(g, T, topo, core, [cores[s] for s in near], src, T["land%d" % x][:, r * w:(r + 1) * w],
+                         T.sem["arr%d_%d" % (x, r)], offc)
+        sent[0] += len(on) + len(offc)
+
+        def go():
+            g.remote_dma_fused(trs, local_sem=T.sem.sent)
+            g.remote_dma_fused([tr], local_sem=T.sem.sent)
+        op("g", go, ["msg%d" % x], ["out%d" % x], (), ("sent", sent[0]))
+
+    def tabtok(s, par):
+        return "tab%d_%d" % (s, par)
+    alltab = [tabtok(s, par) for s in range(N) for par in range(2)]
+
+    def take(x, s):
+        w = width(x)
+        if s == r:
+            src, tok = T["msg%d" % x][:, :], "msg%d" % x
+        else:
+            src, tok = T["land%d" % x][:, s * w:(s + 1) * w], "land%d_%d" % (x, s)
+            n_eng = len(topo.engines(cores[s], cores[plan[s][0][0]]))
+            op("x", None, (), [tok], (), ("arr%d_%d" % (x, s), n_eng))
+        if x == 0:
+            ts(T.tab[:, s * P:(s + 1) * P], src, -7.5, None, A.add, None, [tok], [tabtok(s, 0), tabtok(s, 1)])
+        else:
+            par = (x - 1) % 2
+            ts(T.tab[:, s * P + par:(s + 1) * P:2], src, -7.5, None, A.add, None, [tok], [tabtok(s, par)])
+
+    def own_ints(t):
+        if t < 2:
+            return T.kin_i[:, t:P:2], "kin"
+        return T.ui[:, :], "ui"
+
+    def prep_first(t):
+        if t >= 2:
+            cp(T.ui[:, :], T["msg%d" % (t - 1)][:, :], ["msg%d" % (t - 1)], ["ui"])
+        u, tok = own_ints(t)
+        ts(T.tmpi[:, 0:E], u, 4, None, A.logical_shift_right, None, [tok], ["tmp0"])
+
+    def prep_rest(t):
+        u, tok = own_ints(t)
+        ts(T.n16[:, :], u, 65520, None, A.bitwise_and, None, [tok], ["n16"])
+        cp(T.off[:, :], T.tmpi[:, 0:E], ["tmp0"], ["off"])
+        ts(T.tmpi[:, E:2 * E], u, 15, None, A.bitwise_and, None, [tok], ["tmp1"])
+        for j in range(4):
+            ts(T.tmpi[:, (2 + j) * E:(3 + j) * E], u, 1 << j, None, A.bitwise_and, None, [tok], ["tmp%d" % (2 + j)])
+        ts(T.ma[:, :], T.tmpi[:, E:2 * E], -7.5, None, A.add, None, ["tmp1"], ["ma"])
+        for h, b in enumerate("fg"):
+            ts(T["ps" + b][:, :], T.tmpi[:, (2 + 2 * h) * E:(4 + 2 * h) * E], 2.0, 1.0, A.mult, A.add,
+               ["tmp%d" % (2 + 2 * h), "tmp%d" % (3 + 2 * h)], ["A" + b], [b])
+
+    op("y", lambda: g.sync.dma_start(T.kin_i[:, :], T.kin[:, :]).then_inc(T.sem.loaded, 16), (), ["kin"], (), ("loaded", 16))
+    ms(T.one[:, :], 1.0, ["one"])
+    ms(T.lraw[:, :], math.log(2.0), ["lraw"])
+    ms(T.rp[:, :], 0.0, ["rp"])
+    ms(T.vn[:, :], -1.0 / 256, ["vn"])
+    ms(T.vz[:, :], 2.0 / 256, ["vz"])
+    for j in range(4):
+        ms(T.wm[32 * j:32 * (j + 1), :], 2.0 ** (j - 1) / 32, ["wm%d" % j])
+    ms(T.rp[:, 15:144:16], 2.0, ["rp"])
+    cp(T.msg0[:, :], T.kin_i[:, :], ["kin"], ["msg0"])
+    send(0)
+    asel(T.id32[:, :], [[-1, 128]], A.is_equal, 0.0, 0, 1, "id32", T.one[:, :], "one")
+    asel(T.rp[:, :], [[-1, 144]], A.is_ge, 0.0, 15, 1, "rp")
+    asel(T.rp[:, :], [[1, 144]], A.is_ge, 0.0, 0, -1, "rp")
+    op("g", lambda: g.iota(T.a16[:, :], [[16, P]], 16 * P * r, 0, allow_small_or_imprecise_dtypes=True), (), ["a16"])
+    asel(T.lraw[:, :], [[1, 128]], A.is_gt, -math.log(32.0), 0, -1, "lraw")
+    asel(T.lraw[:, :], [[1, 128]], A.not_equal, -200.0, 0, -1, "lraw")
+    asel(T.lraw[:, :], [[-16, 8], [0, 16]], A.is_ge, -200.0, 0, 1, "lraw")
+    asel(T.lraw[:, :], [[16, 8], [0, 16]], A.is_ge, -200.0, 15, -1, "lraw")
+    act(T.tri[:, :], T.lraw[:, :], F.Exp, 0.0, 1.0, ["lraw"], ["tri"])
+    prep_first(0)
+    take(0, r)
+    prep_rest(0)
+    for t in range(RO):
+        q0 = 17 * t + 3
+        ts(T.sel[:, 128 * t:128 * (t + 1)], T.one[:, :], T.id32[:, q0:q0 + 1], None, A.mult, None, ["one", "id32"], ["sel%d" % t])
+    for i, x in enumerate(IDS):
+        ts(T.ids[:, 128 * i:128 * (i + 1)], T.id32[:, :], x, None, A.mult, None, ["id32"], ["ids"])
+    for s in senders:
+        take(0, s)
+
+    H = E // 2
+    for t in range(RO):
+        par = t % 2
+        own_cols = T.tab[:, r * P + par:(r + 1) * P:2]
+        last = t == RO - 1
+
+        def gather(e, lo, hi):
+            src = T.tab[:, :].indirect(T.off[:, lo:hi])
+            out = T.gat[:, 16 * lo:16 * hi]
+            toks = ["gat%d" % i for i in range(lo // 32, hi // 32)]
+            if e == "v":
+                cp(out, src, alltab + ["off"], toks)
+            else:
+                act(out, src, F.Identity, 0.0, 1.0, alltab + ["off"], toks)
+
+        def gtok(c):
+            return ["gat%d" % i for i in range(4 * c, 4 * c + 4)]
+
+        def braw(c):
+            b = "bc"[c]
+            mm(T["ps" + b][:, 0:H], T.sel[:, 128 * t:128 * (t + 1)], T.gat[:, 2048 * c + t:2048 * (c + 1):16], True, True,
+               gtok(c) + ["sel%d" % t], ["W%s0" % b], [b])
+
+        def bmake(c):
+            b = "bc"[c]
+            ts(T.psh[:, c * H:(c + 1) * H], T["ps" + b][:, 0:H], MAGIC, MAGIC, A.add, A.subtract, ["W%s0" % b], ["B%d" % c], [b, "h"])
+
+        def emake(c):
+            tt(T.e16[:, c * H:(c + 1) * H], T.psh[:, c * H:(c + 1) * H], T.n16[:, c * H:(c + 1) * H], A.subtract,
+               ["B%d" % c, "n16"], ["e16_%d" % c], ["h"])
+
+        def ownmake(c):
+            sl = slice(c * H, (c + 1) * H)
+            act(T.eabs[:, sl], T.e16[:, sl], F.Abs, 0.0, 1.0, ["e16_%d" % c], ["eabs%d" % c])
+            act(T.nown[:, sl], T.eabs[:, sl], F.Sign, -8.0, 1.0, ["eabs%d" % c], ["nown%d" % c])
+            act(T.mul[:, sl], T.nown[:, sl], F.Identity, (1 + 1 / 4096) / 2, (1 - 1 / 4096) / 2, ["nown%d" % c], ["mul%d" % c])
+
+        def subs(c, kq):
+            for k in range(4 * kq, 4 * kq + 4):
+                o = 2048 * c + H * k
+                tt(T.dif[:, o:o + H], T.gat[:, 2048 * c + k:2048 * (c + 1):16], T.psh[:, c * H:(c + 1) * H], A.subtract,
+                   gtok(c) + ["B%d" % c], ["d%d_%d" % (c, k)], ["h"])
+
+        def clamp(c, kq):
+            o = 2048 * c + 4 * H * kq
+            toks = ["d%d_%d" % (c, k) for k in range(4 * kq, 4 * kq + 4)]
+            ts(T.dif[:, o:o + 4 * H], T.dif[:, o:o + 4 * H], -8.0, 8.0, A.max, A.min, toks, toks)
+
+        def sclamp(c, kq):
+            o = 2048 * c + 4 * H * kq
+            toks = ["d%d_%d" % (c, k) for k in range(4 * kq, 4 * kq + 4)]
+            act(T.dif[:, o:o + 4 * H], T.dif[:, o:o + 4 * H], F.Relu, 8.0, -1.0, toks, toks)
+            act(T.dif[:, o:o + 4 * H], T.dif[:, o:o + 4 * H], F.Relu, 16.0, -1.0, toks, toks)
+
+        def reduce4(c, kq, st=False, sp=False):
+            for k in range(4 * kq, 4 * kq + 4):
+                o = 2048 * c + H * k
+                mm(T.psa[:, c * H:(c + 1) * H], T.rp[:, 15 - k:143 - k], T.dif[:, o:o + H], st and k % 4 == 0, sp and k % 4 == 3,
+                   ["d%d_%d" % (c, k), "rp"], ["P%d" % c], ["a"])
+
+        def ownadd(c):
+            mm(T.psa[:, c * H:(c + 1) * H], ident(-5120.0), T.nown[:, c * H:(c + 1) * H], False, False,
+               ["nown%d" % c, "ids"], ["P%d" % c], ["a"])
+
+        def key(x, rhs, toks, st=False, sp=False):
+            mm(T.psd[:, 0:E], ident(x), rhs, st, sp, toks + ["ids"], ["key"], ["d"])
+
+        gather("v", 0, 64)
+        gather("s", 64, 128)
+        gather("v", 128, 160)
+        gather("s", 160, 256)
+        braw(0)
+        bmake(0)
+        subs(0, 0)
+        emake(0)
+        subs(0, 1)
+        clamp(0, 0)
+        reduce4(0, 0, st=True)
+        braw(1)
+        ownmake(0)
+        subs(0, 2)
+        clamp(0, 1)
+        reduce4(0, 1)
+        sclamp(0, 2)
+        subs(0, 3)
+        bmake(1)
+        clamp(0, 3)
+        reduce4(0, 3)
+        ownadd(0)
+        emake(1)
+        subs(1, 0)
+        reduce4(0, 2, sp=True)
+        ownmake(1)
+        sclamp(1, 0)
+        mm(T.pse[:, 0:E], T.id32[:, :], T.e16[:, :], True, False, ["id32", "e16_0", "e16_1"], ["delta"], ["e"])
+        mm(T.pse[:, 0:E], ident(-1.0), T.ma[:, :], False, False, ["ids", "ma"], ["delta"], ["e"])
+        subs(1, 1)
+        subs(1, 2)
+        clamp(1, 1)
+        reduce4(1, 1, st=True)
+        key(-4.5, T.nown[:, :], ["nown0", "nown1"], st=True)
+        ownadd(1)
+        subs(1, 3)
+        clamp(1, 2)
+        reduce4(1, 0)
+        reduce4(1, 2)
+        clamp(1, 3)
+        reduce4(1, 3, sp=True)
+        if last:
+            act(T.yo[:, 1 - par:P:2], T.tab[:, r * P + 1 - par:(r + 1) * P:2], F.Identity, 7.5, 1.0, [tabtok(r, 1 - par)], ["yo1"])
+        tt(T.skip[:, :], T.psh[:, 0:E], T.a16[:, par:P:2], A.is_equal, ["B0", "B1", "a16"], ["skip"], ["h"])
+        key(-60.0, T.skip[:, :], ["skip"])
+        tt(T.pi[:, :], T.psa[:, 0:E], T.mul[:, :], A.mult, ["P0", "P1", "mul0", "mul1"], ["pi"], ["a"])
+
+        def col(buf, j):
+            return buf[:, j * E:(j + 1) * E]
+
+        def wreg(j):
+            b = "bc"[j // 2]
+            return T["ps" + b][:, (j % 2) * E:(j % 2 + 1) * E], "W%s%d" % (b, j % 2), b
+
+        def umake(j):
+            ts(col(T.uu, j), T.pi[:, :], 1 + (2 << j), None, A.bitwise_and, None, ["pi"], ["u%d" % j])
+
+        def zmake(j):
+            b = "fg"[j // 2]
+            tt(col(T.zz, j), col(T.uu, j), T["ps" + b][:, (j % 2) * E:(j % 2 + 1) * E], A.is_equal,
+               ["u%d" % j, "A" + b], ["z%d" % j], [b])
+
+        def vote(j, part):
+            w, tok, b = wreg(j)
+            if part == 0:
+                mm(w, T.vn[:, :], T.tes[:, :], True, False, ["vn", "tes"], [tok], [b])
+            else:
+                mm(w, T.vz[:, :], col(T.zz, j), False, True, ["vz", "z%d" % j], [tok], [b])
+
+        def sign(j):
+            w, tok, b = wreg(j)
+            lo = (j % 2) * E
+            act(T.om[32 * j:32 * (j + 1), :], T["ps" + b][32 * j:32 * (j + 1), lo:lo + E], F.Sign, 1 - 1 / 512, -1.0,
+                [tok], ["om%d" % j], [b])
+
+        def gmake(j):
+            w, tok, b = wreg(j)
+            tt(col(T.gg, j), col(T.zz, j), w, A.is_gt, ["z%d" % j, tok], ["g%d" % j], [b])
+
+        umake(2)
+        umake(3)
+        ts(T.tes[:, :], col(T.uu, 2), 0.0, 2.0, A.is_gt, A.subtract, ["u2"], ["tes"])
+        vote(2, 0)
+        zmake(2)
+        vote(2, 1)
+        vote(3, 0)
+        zmake(3)
+        vote(3, 1)
+        vote(0, 0)
+        key(40.0, T.tes[:, :], ["tes"])
+        sign(2)
+        sign(3)
+        umake(0)
+        umake(1)
+        zmake(0)
+        vote(0, 1)
+        vote(1, 0)
+        zmake(1)
+        vote(1, 1)
+        key(-1.0, col(T.zz, 2), ["z2"])
+        key(-1.0, col(T.zz, 3), ["z3"])
+        sign(0)
+        sign(1)
+        gmake(2)
+        gmake(3)
+        key(-1.0, col(T.zz, 0), ["z0"])
+        key(-1.0, col(T.zz, 1), ["z1"])
+        key(2.0, col(T.gg, 2), ["g2"])
+        key(2.0, col(T.gg, 3), ["g3"])
+        gmake(0)
+        gmake(1)
+        key(2.0, col(T.gg, 0), ["g0"])
+        key(2.0, col(T.gg, 1), ["g1"], sp=True)
+        mm(T.pse[:, 0:E], T.wm[:, :], T.om[:, :], False, True, ["wm%d" % j for j in range(4)] + ["om%d" % j for j in range(4)],
+           ["delta"], ["e"])
+        act(T.xx[:, :], T.psd[:, 0:E], F.Exp, 84.5 * LN64 - 40.0 * LN64, LN64, ["key"], ["xx"], ["d"])
+        if not last:
+            prep_first(t + 1)
+        mm(T.pse[:, E:2 * E], T.tri[:, :], T.xx[:, :], True, True, ["tri", "xx"], ["tsum"], ["e"])
+        tt(T.win[:, :], T.pse[:, E:2 * E], T.xx[:, :], A.is_lt, ["tsum", "xx"], ["win"], ["e"])
+        tt(T.psh[:, E:2 * E], T.pse[:, 0:E], T.win[:, :], A.mult, ["delta", "win"], ["tt"], ["e", "h"])
+        tt(T.ss[:, :], T.psh[:, E:2 * E], own_cols, A.add, ["tt", tabtok(r, par)], ["ss"], ["h"])
+        if last:
+            ts(T.yo[:, par:P:2], T.ss[:, :], 7.5, None, A.add, None, ["ss"], ["yo0"])
+            op("y", lambda: g.sync.dma_start(T.yk[:, :], T.yo[:, :]).then_inc(T.sem.stored, 16), ["yo0", "yo1"], ["yk"], (),
+               ("stored", 16))
+        else:
+            ts(T["msg%d" % (t + 1)][:, :], T.ss[:, :], 7.5, None, A.add, None, ["ss"], ["msg%d" % (t + 1)])
+            send(t + 1)
+            take(t + 1, r)
+            prep_rest(t + 1)
+            for s in senders:
+                take(t + 1, s)
+    op("y", None, ["yk"], ())
+    op("g", None, ["out%d" % (RO - 1)], ())
+    emit(g, T, ops)

@@ -52,8 +52,13 @@ for _t in range(1, RO):
 for _b in "abcdefgh":
     SCRATCH["ps" + _b] = ("psum", [128, 512], "float32")
 
-SEMAPHORES = (["sv", "ss", "sp", "sg", "loaded", "stored", "sent"] + ["rin%d" % t for t in range(RO)]
-              + ["arr%d_%d" % (t, r) for t in range(RO) for r in range(N)])
+MSGS = [(0, 0, P)] + [(x, 0, E) for x in range(1, RO)]
+C = 128
+PIECE = [(0, E)]
+CHUNKS = [[0, 1]]
+
+SEMAPHORES = (["sv", "ss", "sp", "sg", "loaded", "stored", "sent"] + ["rin%d" % m for m in range(len(MSGS))]
+              + ["arr%d_%d" % (m, r) for m in range(len(MSGS)) for r in range(N)])
 
 
 def bits(engs):
@@ -94,13 +99,13 @@ def helper_program(g, core, T, topo, r, dsts):
     cores = list(T.cores)
     n_in = len(topo.engines(cores[r], core)) // 2
     engs = topo.engines(core, cores[dsts[0]])
-    for x in range(RO):
-        w = width(x)
-        g.wait_ge(T.sem["rin%d" % x], n_in)
-        tr = one_to_many(g, T, topo, core, [cores[s] for s in dsts], T["msg%d" % x][:, :],
-                         T["land%d" % x][:, r * w:(r + 1) * w], T.sem["arr%d_%d" % (x, r)], engs)
+    for m, (x, lo, n) in enumerate(MSGS):
+        o = r * width(x) + lo
+        g.wait_ge(T.sem["rin%d" % m], n_in)
+        tr = one_to_many(g, T, topo, core, [cores[s] for s in dsts], T["msg%d" % x][:, lo:lo + n],
+                         T["land%d" % x][:, o:o + n], T.sem["arr%d_%d" % (m, r)], engs)
         g.remote_dma_fused([tr], local_sem=T.sem.sent)
-    g.wait_ge(T.sem.sent, RO * len(engs))
+    g.wait_ge(T.sem.sent, len(MSGS) * len(engs))
 
 
 def emit(g, T, ops):
@@ -221,39 +226,42 @@ def rank_program(g, core, T, topo):
 
     sent = [0]
 
-    def send(x):
-        w = width(x)
-        src = T["msg%d" % x][:, :]
+    def send(m):
+        x, lo, n = MSGS[m]
+        o = r * width(x) + lo
+        src = T["msg%d" % x][:, lo:lo + n]
         on = topo.engines(core, hs[0])
         h = len(on) // 2
-        trs = [one_to_many(g, T, topo, core, [hs[i]], src, src, T.sem["rin%d" % x], on[i * h:(i + 1) * h]) for i in range(2)]
+        trs = [one_to_many(g, T, topo, core, [hs[i]], src, src, T.sem["rin%d" % m], on[i * h:(i + 1) * h]) for i in range(2)]
         offc = topo.engines(core, cores[near[0]])
-        tr = one_to_many(g, T, topo, core, [cores[s] for s in near], src, T["land%d" % x][:, r * w:(r + 1) * w],
-                         T.sem["arr%d_%d" % (x, r)], offc)
+        tr = one_to_many(g, T, topo, core, [cores[s] for s in near], src, T["land%d" % x][:, o:o + n],
+                         T.sem["arr%d_%d" % (m, r)], offc)
         sent[0] += len(on) + len(offc)
 
         def go():
             g.remote_dma_fused(trs, local_sem=T.sem.sent)
             g.remote_dma_fused([tr], local_sem=T.sem.sent)
-        op("g", go, ["msg%d" % x], ["out%d" % x], (), ("sent", sent[0]))
+        op("g", go, ["msg%d" % m], ["out%d" % m], (), ("sent", sent[0]))
 
-    def tabtok(s, par):
-        return "tab%d_%d" % (s, par)
-    alltab = [tabtok(s, par) for s in range(N) for par in range(2)]
+    def tabtok(s, par, h):
+        return "tab%d_%d_%d" % (s, par, h)
+    alltab = [tabtok(s, par, h) for s in range(N) for par in range(2) for h in range(2)]
 
-    def take(x, s):
-        w = width(x)
+    def take(m, s):
+        x, lo, n = MSGS[m]
         if s == r:
-            src, tok = T["msg%d" % x][:, :], "msg%d" % x
+            src, tok = T["msg%d" % x][:, lo:lo + n], "msg%d" % m
         else:
-            src, tok = T["land%d" % x][:, s * w:(s + 1) * w], "land%d_%d" % (x, s)
+            o = s * width(x) + lo
+            src, tok = T["land%d" % x][:, o:o + n], "land%d_%d" % (m, s)
             n_eng = len(topo.engines(cores[s], cores[plan[s][0][0]]))
-            op("x", None, (), [tok], (), ("arr%d_%d" % (x, s), n_eng))
+            op("x", None, (), [tok], (), ("arr%d_%d" % (m, s), n_eng))
         if x == 0:
-            ts(T.tab[:, s * P:(s + 1) * P], src, -7.5, None, A.add, None, [tok], [tabtok(s, 0), tabtok(s, 1)])
+            ts(T.tab[:, s * P:(s + 1) * P], src, -7.5, None, A.add, None, [tok], [tabtok(s, a, b) for a in range(2) for b in range(2)])
         else:
             par = (x - 1) % 2
-            ts(T.tab[:, s * P + par:(s + 1) * P:2], src, -7.5, None, A.add, None, [tok], [tabtok(s, par)])
+            o = s * P + 2 * lo
+            ts(T.tab[:, o + par:o + 2 * n:2], src, -7.5, None, A.add, None, [tok], [tabtok(s, par, 0), tabtok(s, par, 1)])
 
     def own_ints(t):
         if t < 2:
@@ -263,11 +271,14 @@ def rank_program(g, core, T, topo):
     def prep_first(t):
         if t >= 2:
             cp(T.ui[:, :], T["msg%d" % (t - 1)][:, :], ["msg%d" % (t - 1)], ["ui"])
-        u, tok = own_ints(t)
-        ts(T.tmpi[:, 0:E], u, 4, None, A.logical_shift_right, None, [tok], ["tmp0"])
+        else:
+            u, tok = own_ints(t)
+            ts(T.tmpi[:, 0:E], u, 4, None, A.logical_shift_right, None, [tok], ["tmp0"])
 
     def prep_rest(t):
         u, tok = own_ints(t)
+        if t >= 2:
+            ts(T.tmpi[:, 0:E], u, 4, None, A.logical_shift_right, None, [tok], ["tmp0"])
         ts(T.n16[:, :], u, 65520, None, A.bitwise_and, None, [tok], ["n16"])
         cp(T.off[:, :], T.tmpi[:, 0:E], ["tmp0"], ["off"])
         ts(T.tmpi[:, E:2 * E], u, 15, None, A.bitwise_and, None, [tok], ["tmp1"])
@@ -309,63 +320,175 @@ def rank_program(g, core, T, topo):
     for s in senders:
         take(0, s)
 
-    H = E // 2
+    H, G = C, 16 * C
     for t in range(RO):
         par = t % 2
-        own_cols = T.tab[:, r * P + par:(r + 1) * P:2]
         last = t == RO - 1
 
         def gather(e, lo, hi):
             src = T.tab[:, :].indirect(T.off[:, lo:hi])
             out = T.gat[:, 16 * lo:16 * hi]
-            toks = ["gat%d" % i for i in range(lo // 32, hi // 32)]
+            toks = ["gat%d" % i for i in range(lo // 8, hi // 8)]
             if e == "v":
                 cp(out, src, alltab + ["off"], toks)
             else:
                 act(out, src, F.Identity, 0.0, 1.0, alltab + ["off"], toks)
 
         def gtok(c):
-            return ["gat%d" % i for i in range(4 * c, 4 * c + 4)]
+            return ["gat%d" % i for i in range(16 * c, 16 * c + 16)]
 
         def braw(c):
-            b = "bc"[c]
-            mm(T["ps" + b][:, 0:H], T.sel[:, 128 * t:128 * (t + 1)], T.gat[:, 2048 * c + t:2048 * (c + 1):16], True, True,
-               gtok(c) + ["sel%d" % t], ["W%s0" % b], [b])
+            b = "bc"[c % 2]
+            mm(T["ps" + b][:, E - H:E], T.sel[:, 128 * t:128 * (t + 1)], T.gat[:, G * c + t:G * (c + 1):16], True, True,
+               gtok(c) + ["sel%d" % t], ["W%s0_0" % b], [b])
 
         def bmake(c):
-            b = "bc"[c]
-            ts(T.psh[:, c * H:(c + 1) * H], T["ps" + b][:, 0:H], MAGIC, MAGIC, A.add, A.subtract, ["W%s0" % b], ["B%d" % c], [b, "h"])
+            b = "bc"[c % 2]
+            ts(T.psh[:, c * H:(c + 1) * H], T["ps" + b][:, E - H:E], MAGIC, MAGIC, A.add, A.subtract, ["W%s0_0" % b], ["B%d" % c], [b, "h"])
 
         def emake(c):
             tt(T.e16[:, c * H:(c + 1) * H], T.psh[:, c * H:(c + 1) * H], T.n16[:, c * H:(c + 1) * H], A.subtract,
                ["B%d" % c, "n16"], ["e16_%d" % c], ["h"])
 
-        def ownmake(c):
-            sl = slice(c * H, (c + 1) * H)
-            act(T.eabs[:, sl], T.e16[:, sl], F.Abs, 0.0, 1.0, ["e16_%d" % c], ["eabs%d" % c])
-            act(T.nown[:, sl], T.eabs[:, sl], F.Sign, -8.0, 1.0, ["eabs%d" % c], ["nown%d" % c])
-            act(T.mul[:, sl], T.nown[:, sl], F.Identity, (1 + 1 / 4096) / 2, (1 - 1 / 4096) / 2, ["nown%d" % c], ["mul%d" % c])
-
-        def subs(c, kq):
-            for k in range(4 * kq, 4 * kq + 4):
-                o = 2048 * c + H * k
-                tt(T.dif[:, o:o + H], T.gat[:, 2048 * c + k:2048 * (c + 1):16], T.psh[:, c * H:(c + 1) * H], A.subtract,
+        def subs(c, kq, ks=range(4)):
+            for k in [4 * kq + i for i in ks]:
+                o = G * c + H * k
+                tt(T.dif[:, o:o + H], T.gat[:, G * c + k:G * (c + 1):16], T.psh[:, c * H:(c + 1) * H], A.subtract,
                    gtok(c) + ["B%d" % c], ["d%d_%d" % (c, k)], ["h"])
 
         def clamp(c, kq):
-            o = 2048 * c + 4 * H * kq
+            o = G * c + 4 * H * kq
             toks = ["d%d_%d" % (c, k) for k in range(4 * kq, 4 * kq + 4)]
             ts(T.dif[:, o:o + 4 * H], T.dif[:, o:o + 4 * H], -8.0, 8.0, A.max, A.min, toks, toks)
 
         def sclamp(c, kq):
-            o = 2048 * c + 4 * H * kq
+            o = G * c + 4 * H * kq
             toks = ["d%d_%d" % (c, k) for k in range(4 * kq, 4 * kq + 4)]
+            sl = slice(c * H, (c + 1) * H)
+            act(T.eabs[:, sl], T.e16[:, sl], F.Abs, 0.0, 1.0, ["e16_%d" % c], ["eabs%d" % c])
             act(T.dif[:, o:o + 4 * H], T.dif[:, o:o + 4 * H], F.Relu, 8.0, -1.0, toks, toks)
+            act(T.nown[:, sl], T.eabs[:, sl], F.Sign, -8.0, 1.0, ["eabs%d" % c], ["nown%d" % c])
             act(T.dif[:, o:o + 4 * H], T.dif[:, o:o + 4 * H], F.Relu, 16.0, -1.0, toks, toks)
+            act(T.mul[:, sl], T.nown[:, sl], F.Identity, (1 + 1 / 4096) / 2, (1 - 1 / 4096) / 2, ["nown%d" % c], ["mul%d" % c])
+
+        def clamp2(c, k, sp=False):
+            o = G * c + H * k
+            toks = ["d%d_%d" % (c, k), "d%d_%d" % (c, k + 1)]
+            ts(T.dif[:, o:o + 2 * H], T.dif[:, o:o + 2 * H], -8.0, 8.0, A.max, A.min, toks, toks)
+            for i in range(2):
+                mm(T.psa[:, c * H:(c + 1) * H], T.rp[:, 15 - k - i:143 - k - i], T.dif[:, o + i * H:o + (i + 1) * H], False,
+                   sp and i == 1, [toks[i], "rp"], ["P%d" % c], ["a"])
+
+        def elect():
+            for c in range(2):
+                tt(T.pi[:, c * H:(c + 1) * H], T.psa[:, c * H:(c + 1) * H], T.mul[:, c * H:(c + 1) * H], A.mult,
+                   ["P%d" % c, "mul%d" % c], ["pi0" if c else "pia"], ["a"])
+            for c in range(2):
+                ts(T.uu[:, 2 * E + c * H:2 * E + (c + 1) * H], T.pi[:, c * H:(c + 1) * H], 1 + (2 << 2), None, A.bitwise_and, None,
+                   ["pi0" if c else "pia"], ["u0_2" if c else "ua"])
+            umake(0, 3)
+            umake(0, 0)
+            ts(col(T.tes, 0), col(T.uu, 0, 2), 0.0, 2.0, A.is_gt, A.subtract, ["u0_2"], ["tes0"])
+            vote(0, 2, 0)
+            zmake(0, 2)
+            vote(0, 2, 1)
+            vote(0, 3, 0)
+            umake(0, 1)
+            zmake(0, 3)
+            vote(0, 3, 1)
+            vote(0, 0, 0)
+            zmake(0, 0)
+            vote(0, 0, 1)
+            vote(0, 1, 0)
+            zmake(0, 1)
+            vote(0, 1, 1)
+            key(0, 40.0, T.tes, 0, ["tes0"])
+            gmake(0, 2)
+            gmake(0, 3)
+            for j in (2, 3, 0, 1):
+                key(0, -1.0, T.zz, j, ["z0_%d" % j])
+            sign(0, 2)
+            sign(0, 3)
+            gmake(0, 0)
+            gmake(0, 1)
+            for j in (2, 3, 0, 1):
+                key(0, 2.0, T.gg, j, ["g0_%d" % j], sp=j == 1)
+            sign(0, 0)
+            act(col(T.xx, 0), col(T.psd, 0), F.Exp, 44.5 * LN64, LN64, ["key0"], ["xx"], ["d"])
+            sign(0, 1)
+            mm(col(T.psa, 0), T.tri[:, :], col(T.xx, 0), True, True, ["tri", "xx"], ["P0", "P1"], ["a"])
+            mm(col(T.pse, 0), T.wm[:, :], col(T.om, 0), False, True,
+               ["wm%d" % j for j in range(4)] + ["om0_%d" % j for j in range(4)], ["delta0"], ["e"])
+            if not last:
+                prep_first(t + 1)
+            hv = [slice(0, H), slice(H, E)]
+            for c in range(2):
+                tt(T.win[:, hv[c]], T.psa[:, hv[c]], T.xx[:, hv[c]], A.is_lt, ["P%d" % c, "xx"], ["win%d" % c], ["a"])
+            for c in range(2):
+                tt(T.psh[:, E + c * H:E + (c + 1) * H], T.pse[:, hv[c]], T.win[:, hv[c]], A.mult, ["delta0", "win%d" % c], ["tt%d" % c],
+                   ["e", "h"])
+            for c in range(2):
+                o = r * P + 2 * c * H
+                tt(T.ss[:, hv[c]], T.psh[:, E + c * H:E + (c + 1) * H], T.tab[:, o + par:o + 2 * H:2], A.add,
+                   ["tt%d" % c, tabtok(r, par, c)], ["ss%d" % c], ["h"])
+            for c in range(2):
+                if last:
+                    ts(T.yo[:, 2 * c * H + par:2 * (c + 1) * H:2], T.ss[:, hv[c]], 7.5, None, A.add, None, ["ss%d" % c], ["yo%d" % c])
+                else:
+                    ts(T["msg%d" % (t + 1)][:, hv[c]], T.ss[:, hv[c]], 7.5, None, A.add, None, ["ss%d" % c],
+                       ["msg%s%d" % ("a" if c == 0 else "", t + 1)])
+            if last:
+                op("y", lambda: g.sync.dma_start(T.yk[:, :], T.yo[:, :]).then_inc(T.sem.stored, 16),
+                   ["yo0", "yo1", "yo2"], ["yk1"], (), ("stored", 16))
+            else:
+                send(t + 1)
+
+        def compare():
+            gather("v", 0, 64)
+            gather("s", 64, 128)
+            gather("v", 128, 152)
+            gather("s", 160, 256)
+            braw(0)
+            bmake(0)
+            gather("v", 152, 160)
+            subs(0, 0)
+            emake(0)
+            subs(0, 1)
+            clamp(0, 0)
+            reduce4(0, 0, st=True)
+            braw(1)
+            subs(0, 2)
+            clamp(0, 1)
+            reduce4(0, 1)
+            sclamp(0, 2)
+            subs(0, 3)
+            bmake(1)
+            clamp(0, 3)
+            emake(1)
+            subs(1, 0)
+            reduce4(0, 3)
+            ownadd(0)
+            reduce4(0, 2, sp=True)
+            sclamp(1, 0)
+            delta(0)
+            subs(1, 1)
+            subs(1, 2)
+            clamp(1, 1)
+            reduce4(1, 1, st=True)
+            key(0, -4.5, T.nown, 0, ["nown0", "nown1"], st=True)
+            ownadd(1)
+            subs(1, 3, [0, 1])
+            clamp(1, 2)
+            reduce4(1, 2)
+            reduce4(1, 0)
+            subs(1, 3, [2, 3])
+            clamp2(1, 12)
+            clamp2(1, 14, sp=True)
+            skipmake(0)
 
         def reduce4(c, kq, st=False, sp=False):
             for k in range(4 * kq, 4 * kq + 4):
-                o = 2048 * c + H * k
+                o = G * c + H * k
                 mm(T.psa[:, c * H:(c + 1) * H], T.rp[:, 15 - k:143 - k], T.dif[:, o:o + H], st and k % 4 == 0, sp and k % 4 == 3,
                    ["d%d_%d" % (c, k), "rp"], ["P%d" % c], ["a"])
 
@@ -373,142 +496,64 @@ def rank_program(g, core, T, topo):
             mm(T.psa[:, c * H:(c + 1) * H], ident(-5120.0), T.nown[:, c * H:(c + 1) * H], False, False,
                ["nown%d" % c, "ids"], ["P%d" % c], ["a"])
 
-        def key(x, rhs, toks, st=False, sp=False):
-            mm(T.psd[:, 0:E], ident(x), rhs, st, sp, toks + ["ids"], ["key"], ["d"])
+        def key(c, x, buf, j, toks, st=False, sp=False):
+            mm(col(T.psd, c), ident(x), col(buf, c, j), st, sp, toks + ["ids"], ["key%d" % c], ["d"])
 
-        gather("v", 0, 64)
-        gather("s", 64, 128)
-        gather("v", 128, 160)
-        gather("s", 160, 256)
-        braw(0)
-        bmake(0)
-        subs(0, 0)
-        emake(0)
-        subs(0, 1)
-        clamp(0, 0)
-        reduce4(0, 0, st=True)
-        braw(1)
-        ownmake(0)
-        subs(0, 2)
-        clamp(0, 1)
-        reduce4(0, 1)
-        sclamp(0, 2)
-        subs(0, 3)
-        bmake(1)
-        clamp(0, 3)
-        reduce4(0, 3)
-        ownadd(0)
-        emake(1)
-        subs(1, 0)
-        reduce4(0, 2, sp=True)
-        ownmake(1)
-        sclamp(1, 0)
-        mm(T.pse[:, 0:E], T.id32[:, :], T.e16[:, :], True, False, ["id32", "e16_0", "e16_1"], ["delta"], ["e"])
-        mm(T.pse[:, 0:E], ident(-1.0), T.ma[:, :], False, False, ["ids", "ma"], ["delta"], ["e"])
-        subs(1, 1)
-        subs(1, 2)
-        clamp(1, 1)
-        reduce4(1, 1, st=True)
-        key(-4.5, T.nown[:, :], ["nown0", "nown1"], st=True)
-        ownadd(1)
-        subs(1, 3)
-        clamp(1, 2)
-        reduce4(1, 0)
-        reduce4(1, 2)
-        clamp(1, 3)
-        reduce4(1, 3, sp=True)
-        if last:
-            act(T.yo[:, 1 - par:P:2], T.tab[:, r * P + 1 - par:(r + 1) * P:2], F.Identity, 7.5, 1.0, [tabtok(r, 1 - par)], ["yo1"])
-        tt(T.skip[:, :], T.psh[:, 0:E], T.a16[:, par:P:2], A.is_equal, ["B0", "B1", "a16"], ["skip"], ["h"])
-        key(-60.0, T.skip[:, :], ["skip"])
-        tt(T.pi[:, :], T.psa[:, 0:E], T.mul[:, :], A.mult, ["P0", "P1", "mul0", "mul1"], ["pi"], ["a"])
+        def col(buf, c, j=0):
+            return buf[:, j * E + PIECE[c][0]:j * E + PIECE[c][1]]
 
-        def col(buf, j):
-            return buf[:, j * E:(j + 1) * E]
+        def each(name, c):
+            return ["%s%d" % (name, q) for q in CHUNKS[c]]
 
-        def wreg(j):
+        def wreg(c, j):
             b = "bc"[j // 2]
-            return T["ps" + b][:, (j % 2) * E:(j % 2 + 1) * E], "W%s%d" % (b, j % 2), b
+            return col(T["ps" + b], c, j % 2), "W%s%d_%d" % (b, j % 2, c), b
 
-        def umake(j):
-            ts(col(T.uu, j), T.pi[:, :], 1 + (2 << j), None, A.bitwise_and, None, ["pi"], ["u%d" % j])
+        def delta(c):
+            mm(col(T.pse, c), T.id32[:, :], col(T.e16, c), True, False, ["id32"] + each("e16_", c), ["delta%d" % c], ["e"])
+            mm(col(T.pse, c), ident(-1.0), col(T.ma, c), False, False, ["ids", "ma"], ["delta%d" % c], ["e"])
 
-        def zmake(j):
+        def skipmake(c):
+            tt(col(T.skip, c), col(T.psh, c), T.a16[:, 2 * PIECE[c][0] + par:2 * PIECE[c][1]:2], A.is_equal, each("B", c) + ["a16"],
+               ["skip%d" % c], ["h"])
+            key(c, -60.0, T.skip, 0, ["skip%d" % c])
+
+        def umake(c, j):
+            ts(col(T.uu, c, j), col(T.pi, c), 1 + (2 << j), None, A.bitwise_and, None, ["pi%d" % c], ["u%d_%d" % (c, j)])
+
+        def zmake(c, j):
             b = "fg"[j // 2]
-            tt(col(T.zz, j), col(T.uu, j), T["ps" + b][:, (j % 2) * E:(j % 2 + 1) * E], A.is_equal,
-               ["u%d" % j, "A" + b], ["z%d" % j], [b])
+            tt(col(T.zz, c, j), col(T.uu, c, j), col(T["ps" + b], c, j % 2), A.is_equal,
+               ["u%d_%d" % (c, j), "A" + b], ["z%d_%d" % (c, j)], [b])
 
-        def vote(j, part):
-            w, tok, b = wreg(j)
+        def vote(c, j, part):
+            w, tok, b = wreg(c, j)
             if part == 0:
-                mm(w, T.vn[:, :], T.tes[:, :], True, False, ["vn", "tes"], [tok], [b])
+                mm(w, T.vn[:, :], col(T.tes, c), True, False, ["vn", "tes%d" % c], [tok], [b])
             else:
-                mm(w, T.vz[:, :], col(T.zz, j), False, True, ["vz", "z%d" % j], [tok], [b])
+                mm(w, T.vz[:, :], col(T.zz, c, j), False, True, ["vz", "z%d_%d" % (c, j)], [tok], [b])
 
-        def sign(j):
-            w, tok, b = wreg(j)
-            lo = (j % 2) * E
-            act(T.om[32 * j:32 * (j + 1), :], T["ps" + b][32 * j:32 * (j + 1), lo:lo + E], F.Sign, 1 - 1 / 512, -1.0,
-                [tok], ["om%d" % j], [b])
+        def sign(c, j):
+            w, tok, b = wreg(c, j)
+            lo, hi = PIECE[c]
+            o = (j % 2) * E
+            act(T.om[32 * j:32 * (j + 1), lo:hi], T["ps" + b][32 * j:32 * (j + 1), o + lo:o + hi], F.Sign, 1 - 1 / 512, -1.0,
+                [tok], ["om%d_%d" % (c, j)], [b])
 
-        def gmake(j):
-            w, tok, b = wreg(j)
-            tt(col(T.gg, j), col(T.zz, j), w, A.is_gt, ["z%d" % j, tok], ["g%d" % j], [b])
+        def gmake(c, j):
+            w, tok, b = wreg(c, j)
+            tt(col(T.gg, c, j), col(T.zz, c, j), w, A.is_gt, ["z%d_%d" % (c, j), tok], ["g%d_%d" % (c, j)], [b])
 
-        umake(2)
-        umake(3)
-        ts(T.tes[:, :], col(T.uu, 2), 0.0, 2.0, A.is_gt, A.subtract, ["u2"], ["tes"])
-        vote(2, 0)
-        zmake(2)
-        vote(2, 1)
-        vote(3, 0)
-        zmake(3)
-        vote(3, 1)
-        vote(0, 0)
-        key(40.0, T.tes[:, :], ["tes"])
-        sign(2)
-        sign(3)
-        umake(0)
-        umake(1)
-        zmake(0)
-        vote(0, 1)
-        vote(1, 0)
-        zmake(1)
-        vote(1, 1)
-        key(-1.0, col(T.zz, 2), ["z2"])
-        key(-1.0, col(T.zz, 3), ["z3"])
-        sign(0)
-        sign(1)
-        gmake(2)
-        gmake(3)
-        key(-1.0, col(T.zz, 0), ["z0"])
-        key(-1.0, col(T.zz, 1), ["z1"])
-        key(2.0, col(T.gg, 2), ["g2"])
-        key(2.0, col(T.gg, 3), ["g3"])
-        gmake(0)
-        gmake(1)
-        key(2.0, col(T.gg, 0), ["g0"])
-        key(2.0, col(T.gg, 1), ["g1"], sp=True)
-        mm(T.pse[:, 0:E], T.wm[:, :], T.om[:, :], False, True, ["wm%d" % j for j in range(4)] + ["om%d" % j for j in range(4)],
-           ["delta"], ["e"])
-        act(T.xx[:, :], T.psd[:, 0:E], F.Exp, 84.5 * LN64 - 40.0 * LN64, LN64, ["key"], ["xx"], ["d"])
-        if not last:
-            prep_first(t + 1)
-        mm(T.pse[:, E:2 * E], T.tri[:, :], T.xx[:, :], True, True, ["tri", "xx"], ["tsum"], ["e"])
-        tt(T.win[:, :], T.pse[:, E:2 * E], T.xx[:, :], A.is_lt, ["tsum", "xx"], ["win"], ["e"])
-        tt(T.psh[:, E:2 * E], T.pse[:, 0:E], T.win[:, :], A.mult, ["delta", "win"], ["tt"], ["e", "h"])
-        tt(T.ss[:, :], T.psh[:, E:2 * E], own_cols, A.add, ["tt", tabtok(r, par)], ["ss"], ["h"])
+        compare()
         if last:
-            ts(T.yo[:, par:P:2], T.ss[:, :], 7.5, None, A.add, None, ["ss"], ["yo0"])
-            op("y", lambda: g.sync.dma_start(T.yk[:, :], T.yo[:, :]).then_inc(T.sem.stored, 16), ["yo0", "yo1"], ["yk"], (),
-               ("stored", 16))
-        else:
-            ts(T["msg%d" % (t + 1)][:, :], T.ss[:, :], 7.5, None, A.add, None, ["ss"], ["msg%d" % (t + 1)])
-            send(t + 1)
+            act(T.yo[:, 1 - par:P:2], T.tab[:, r * P + 1 - par:(r + 1) * P:2], F.Identity, 7.5, 1.0,
+                [tabtok(r, 1 - par, 0), tabtok(r, 1 - par, 1)], ["yo2"])
+        elect()
+        if not last:
             take(t + 1, r)
             prep_rest(t + 1)
             for s in senders:
                 take(t + 1, s)
-    op("y", None, ["yk"], ())
-    op("g", None, ["out%d" % (RO - 1)], ())
+    op("y", None, ["yk1"], ())
+    op("g", None, ["out%d" % (len(MSGS) - 1)], ())
     emit(g, T, ops)

@@ -5,7 +5,11 @@ from concourse.mybir import AluOpType as A, ActivationFunctionType as F
 N, P, E, RO = 8, 512, 256, 5
 MAGIC = 201326592.0
 LN64 = math.log(64.0)
-IDS = [-1.0, 2.0, 40.0, -4.5, -60.0, -5120.0]
+SHIFT = 32775.5
+H = 128
+BY_SCALAR = [(6, 8), (8, 12), (12, 16), (16, 20), (20, 24), (24, 28), (28, 30), (30, 32)]
+BY_VECTOR = [(0, 2), (2, 4), (4, 6)]
+IDB = [-1.0, 2.0, -2.0, -9.0, 60.0, 40.0]
 
 SCRATCH = {
     "kin_i": ("sbuf", [128, P], "int32"),
@@ -15,15 +19,19 @@ SCRATCH = {
     "gat": ("sbuf", [128, 16 * E], "float32"),
     "dif": ("sbuf", [128, 16 * E], "bfloat16"),
     "off": ("sbuf", [128, E], "uint16"),
-    "ui": ("sbuf", [128, E], "int32"),
-    "tmpi": ("sbuf", [128, 6 * E], "int32"),
-    "n16": ("sbuf", [128, E], "int32"),
+    "turn": ("sbuf", [128, 32], "uint16"),
+    "small": ("sbuf", [128, 128], "int32"),
+    "k16": ("sbuf", [128, 32], "float16"),
+    "nt": ("sbuf", [128, E], "float16"),
+    "nx": ("sbuf", [128, 8 * E], "float16"),
+    "gb": ("sbuf", [128, E], "float16"),
+    "n16": ("sbuf", [128, E], "float16"),
+    "a16": ("sbuf", [128, P], "float16"),
     "ma": ("sbuf", [128, E], "bfloat16"),
-    "e16": ("sbuf", [128, E], "float32"),
-    "eabs": ("sbuf", [128, E], "float32"),
-    "nown": ("sbuf", [128, E], "bfloat16"),
-    "mul": ("sbuf", [128, E], "float32"),
-    "skip": ("sbuf", [128, E], "bfloat16"),
+    "qm": ("sbuf", [128, 5 * E], "bfloat16"),
+    "qc": ("sbuf", [128, 4 * E], "bfloat16"),
+    "sg": ("sbuf", [128, 2 * E], "bfloat16"),
+    "no": ("sbuf", [128, 2 * E], "bfloat16"),
     "pi": ("sbuf", [128, E], "int32"),
     "uu": ("sbuf", [128, 4 * E], "int32"),
     "tes": ("sbuf", [128, E], "bfloat16"),
@@ -32,18 +40,21 @@ SCRATCH = {
     "om": ("sbuf", [128, E], "bfloat16"),
     "xx": ("sbuf", [128, E], "bfloat16"),
     "win": ("sbuf", [128, E], "bfloat16"),
-    "ss": ("sbuf", [128, E], "float32"),
     "yo": ("sbuf", [128, P], "float32"),
-    "a16": ("sbuf", [128, P], "float32"),
+    "a32": ("sbuf", [128, P], "float32"),
     "one": ("sbuf", [128, 128], "float32"),
+    "ones": ("sbuf", [128, E], "bfloat16"),
     "id32": ("sbuf", [128, 128], "float32"),
-    "ids": ("sbuf", [128, 128 * len(IDS)], "bfloat16"),
-    "sel": ("sbuf", [128, 128 * RO], "float32"),
+    "idb": ("sbuf", [128, 128 * len(IDB)], "bfloat16"),
+    "idh": ("sbuf", [128, 128], "float16"),
+    "sel": ("sbuf", [128, 128 * RO], "float16"),
+    "comb": ("sbuf", [128, 144], "bfloat16"),
     "rp": ("sbuf", [128, 144], "bfloat16"),
     "lraw": ("sbuf", [128, 128], "float32"),
     "tri": ("sbuf", [128, 128], "bfloat16"),
-    "vn": ("sbuf", [128, 128], "bfloat16"),
+    "vt": ("sbuf", [128, 128], "bfloat16"),
     "vz": ("sbuf", [128, 128], "bfloat16"),
+    "vk": ("sbuf", [128, 128], "bfloat16"),
     "wm": ("sbuf", [128, 128], "bfloat16"),
 }
 for _t in range(1, RO):
@@ -52,13 +63,17 @@ for _t in range(1, RO):
 for _b in "abcdefgh":
     SCRATCH["ps" + _b] = ("psum", [128, 512], "float32")
 
-MSGS = [(0, 0, P)] + [(x, 0, E) for x in range(1, RO)]
-C = 128
-PIECE = [(0, E)]
-CHUNKS = [[0, 1]]
+NAME = "a"
+CODE = "c"
+RIVAL = "c"
+KEY = "d"
+DELTA = "e"
+MINE = "fg"
+SELF = "h"
+VOTE = "abhf"
 
-SEMAPHORES = (["sv", "ss", "sp", "sg", "loaded", "stored", "sent"] + ["rin%d" % m for m in range(len(MSGS))]
-              + ["arr%d_%d" % (m, r) for m in range(len(MSGS)) for r in range(N)])
+SEMAPHORES = (["sv", "ss", "sp", "sg", "loaded", "stored", "sent"] + ["rin%d" % m for m in range(RO)]
+              + ["arr%d_%d" % (m, r) for m in range(RO) for r in range(N)])
 
 
 def bits(engs):
@@ -99,13 +114,13 @@ def helper_program(g, core, T, topo, r, dsts):
     cores = list(T.cores)
     n_in = len(topo.engines(cores[r], core)) // 2
     engs = topo.engines(core, cores[dsts[0]])
-    for m, (x, lo, n) in enumerate(MSGS):
-        o = r * width(x) + lo
+    for m in range(RO):
+        n = width(m)
         g.wait_ge(T.sem["rin%d" % m], n_in)
-        tr = one_to_many(g, T, topo, core, [cores[s] for s in dsts], T["msg%d" % x][:, lo:lo + n],
-                         T["land%d" % x][:, o:o + n], T.sem["arr%d_%d" % (m, r)], engs)
+        tr = one_to_many(g, T, topo, core, [cores[s] for s in dsts], T["msg%d" % m][:, :],
+                         T["land%d" % m][:, r * n:(r + 1) * n], T.sem["arr%d_%d" % (m, r)], engs)
         g.remote_dma_fused([tr], local_sem=T.sem.sent)
-    g.wait_ge(T.sem.sent, len(MSGS) * len(engs))
+    g.wait_ge(T.sem.sent, RO * len(engs))
 
 
 def emit(g, T, ops):
@@ -187,7 +202,7 @@ def rank_program(g, core, T, topo):
     from_near = sorted(near, key=lambda s: plan[s][0].index(r))
     from_far = sorted([s for s in range(N) if s != r and s not in near],
                       key=lambda s: [d.index(r) for d in plan[s][1].values() if r in d][0])
-    senders = from_near + from_far
+    senders = from_near[:2] + from_far[:2] + from_near[2:] + from_far[2:]
     hs = list(helpers.keys())
     V, S, PE = g.vector, g.scalar, g.tensor
     ops = []
@@ -213,347 +228,276 @@ def rank_program(g, core, T, topo):
     def act(out, in_, f, bias, scale, rd, wr, bk=()):
         op("s", lambda: S.activation(out, in_, f, bias=bias, scale=scale), rd, wr, bk)
 
-    def mm(out, lhsT, rhs, st, sp, rd, wr, bk):
-        op("p", lambda: PE.matmul(out, lhsT, rhs, st, sp), rd, wr, bk)
+    def mm(bank, lo, hi, lhsT, rhs, st, sp, rd, step=1):
+        out = T["ps" + bank][:, lo:hi] if step == 1 else T["ps" + bank][:, lo:hi:step]
+        op("p", lambda: PE.matmul(out, lhsT, rhs, st, sp), rd, ["ps" + bank], [bank])
 
     def asel(ap, pat, cmp, fill, base, cm, tok, src=None, srctok=None):
         op("g", lambda: g.affine_select(ap, ap if src is None else src, pat, cmp, fill, base, cm),
            [tok if srctok is None else srctok], [tok])
 
-    def ident(x):
-        i = IDS.index(x)
-        return T.ids[:, 128 * i:128 * (i + 1)]
+    def idb(x):
+        i = IDB.index(x)
+        return T.idb[:, 128 * i:128 * (i + 1)]
+
+    def ps(bank, lo, hi):
+        return T["ps" + bank][:, lo:hi]
 
     sent = [0]
 
-    def send(m):
-        x, lo, n = MSGS[m]
-        o = r * width(x) + lo
-        src = T["msg%d" % x][:, lo:lo + n]
+    def send(m, toks):
+        n = width(m)
+        src = T["msg%d" % m][:, :]
         on = topo.engines(core, hs[0])
         h = len(on) // 2
         trs = [one_to_many(g, T, topo, core, [hs[i]], src, src, T.sem["rin%d" % m], on[i * h:(i + 1) * h]) for i in range(2)]
         offc = topo.engines(core, cores[near[0]])
-        tr = one_to_many(g, T, topo, core, [cores[s] for s in near], src, T["land%d" % x][:, o:o + n],
+        tr = one_to_many(g, T, topo, core, [cores[s] for s in near], src, T["land%d" % m][:, r * n:(r + 1) * n],
                          T.sem["arr%d_%d" % (m, r)], offc)
         sent[0] += len(on) + len(offc)
 
         def go():
             g.remote_dma_fused(trs, local_sem=T.sem.sent)
             g.remote_dma_fused([tr], local_sem=T.sem.sent)
-        op("g", go, ["msg%d" % m], ["out%d" % m], (), ("sent", sent[0]))
+        op("g", go, toks, ["out%d" % m], (), ("sent", sent[0]))
 
-    def tabtok(s, par, h):
-        return "tab%d_%d_%d" % (s, par, h)
-    alltab = [tabtok(s, par, h) for s in range(N) for par in range(2) for h in range(2)]
+    def owntok(par, c):
+        return "own%d_%d" % (par, c)
+    allown = [owntok(par, c) for par in range(2) for c in range(2)]
+    alltab = ["tab%d" % s for s in range(N) if s != r] + allown
+
+    def own(par, lo=0, hi=E):
+        return T.tab[:, r * P + 2 * lo + par:r * P + 2 * hi:2]
+
+    def plane(buf, i, k=1):
+        return buf[:, i * E:(i + k) * E]
 
     def take(m, s):
-        x, lo, n = MSGS[m]
-        if s == r:
-            src, tok = T["msg%d" % x][:, lo:lo + n], "msg%d" % m
-        else:
-            o = s * width(x) + lo
-            src, tok = T["land%d" % x][:, o:o + n], "land%d_%d" % (m, s)
-            n_eng = len(topo.engines(cores[s], cores[plan[s][0][0]]))
-            op("x", None, (), [tok], (), ("arr%d_%d" % (m, s), n_eng))
-        if x == 0:
-            ts(T.tab[:, s * P:(s + 1) * P], src, -7.5, None, A.add, None, [tok], [tabtok(s, a, b) for a in range(2) for b in range(2)])
-        else:
-            par = (x - 1) % 2
-            o = s * P + 2 * lo
-            ts(T.tab[:, o + par:o + 2 * n:2], src, -7.5, None, A.add, None, [tok], [tabtok(s, par, 0), tabtok(s, par, 1)])
+        n = width(m)
+        tok = "land%d_%d" % (m, s)
+        op("x", None, (), [tok], (), ("arr%d_%d" % (m, s), len(topo.engines(cores[s], cores[plan[s][0][0]]))))
+        out = T.tab[:, s * P:(s + 1) * P] if m == 0 else T.tab[:, s * P + (m - 1) % 2:(s + 1) * P:2]
+        ts(out, T["land%d" % m][:, s * n:(s + 1) * n], -SHIFT, None, A.add, None, [tok], ["tab%d" % s])
 
-    def own_ints(t):
-        if t < 2:
-            return T.kin_i[:, t:P:2], "kin"
-        return T.ui[:, :], "ui"
+    def offsets(t):
+        src = T.tab[:, r * P:(r + 1) * P].indirect(T.turn[:, 16 * (t % 2):16 * (t % 2) + 16])
+        steps = [lambda: ts(T.nt[:, :], src, MAGIC, MAGIC, A.add, A.subtract, allown + ["turn"], ["nt"])]
+        for x in range(8):
+            steps.append(lambda x=x: ts(plane(T.nx, x), T.nt[:, :], T.rp[:, 16 * x + 15:16 * x + 16], 0.5, A.mult, A.mult, ["nt", "rp"], ["nx%d" % x]))
 
-    def prep_first(t):
-        if t >= 2:
-            cp(T.ui[:, :], T["msg%d" % (t - 1)][:, :], ["msg%d" % (t - 1)], ["ui"])
-        else:
-            u, tok = own_ints(t)
-            ts(T.tmpi[:, 0:E], u, 4, None, A.logical_shift_right, None, [tok], ["tmp0"])
+        def turn():
+            for e1 in range(16):
+                mm(SELF, e1, E, T.nx[:, e1:8 * E:16], T.k16[:, t:t + 16], True, True, ["k16"] + ["nx%d" % x for x in range(8)], 16)
+        return steps + [turn, lambda: ts(T.off[:, :], ps(SELF, 0, E), 2048.0, None, A.add, None, ["ps" + SELF], ["off"], [SELF])]
 
-    def prep_rest(t):
-        u, tok = own_ints(t)
-        if t >= 2:
-            ts(T.tmpi[:, 0:E], u, 4, None, A.logical_shift_right, None, [tok], ["tmp0"])
-        ts(T.n16[:, :], u, 65520, None, A.bitwise_and, None, [tok], ["n16"])
-        cp(T.off[:, :], T.tmpi[:, 0:E], ["tmp0"], ["off"])
-        ts(T.tmpi[:, E:2 * E], u, 15, None, A.bitwise_and, None, [tok], ["tmp1"])
-        for j in range(4):
-            ts(T.tmpi[:, (2 + j) * E:(3 + j) * E], u, 1 << j, None, A.bitwise_and, None, [tok], ["tmp%d" % (2 + j)])
-        ts(T.ma[:, :], T.tmpi[:, E:2 * E], -7.5, None, A.add, None, ["tmp1"], ["ma"])
-        for h, b in enumerate("fg"):
-            ts(T["ps" + b][:, :], T.tmpi[:, (2 + 2 * h) * E:(4 + 2 * h) * E], 2.0, 1.0, A.mult, A.add,
-               ["tmp%d" % (2 + 2 * h), "tmp%d" % (3 + 2 * h)], ["A" + b], [b])
+    def prepare(t):
+        par = t % 2
+        mine = [owntok(par, 0), owntok(par, 1)]
+        ts(T.n16[:, :], own(par), MAGIC, MAGIC, A.add, A.subtract, mine, ["n16"])
+        mm(DELTA, 0, E, T.id32[:, :], own(par), True, False, ["id32"] + mine)
+        mm(DELTA, 0, E, T.idh[:, :], T.n16[:, :], False, True, ["idh", "n16"])
+        for i in range(4):
+            bias = 199.5 if i == 0 else 191.5 * 2 ** i + 8
+            act(plane(T.qm, i), ps(DELTA, 0, E), F.Identity, bias, 1.0, ["ps" + DELTA], ["qm%d" % i], [DELTA])
+        act(T.ma[:, :], ps(DELTA, 0, E), F.Identity, 7.5, 1.0, ["ps" + DELTA], ["ma"], [DELTA])
+        for h, b in enumerate(MINE):
+            mm(b, 0, 2 * E, idb(2.0), plane(T.qc, 2 * h, 2), True, False, ["qc%d" % (2 * h), "qc%d" % (2 * h + 1)])
+            mm(b, 0, 2 * E, idb(2.0), plane(T.qm, 2 * h, 2), False, False, ["qm%d" % (2 * h), "qm%d" % (2 * h + 1)])
+            mm(b, 0, 2 * E, idb(-2.0), plane(T.qm, 2 * h + 1, 2), False, True, ["qm%d" % (2 * h + 1), "qm%d" % (2 * h + 2)])
 
     op("y", lambda: g.sync.dma_start(T.kin_i[:, :], T.kin[:, :]).then_inc(T.sem.loaded, 16), (), ["kin"], (), ("loaded", 16))
+    op("g", lambda: g.iota(T.small[:, 0:32], [[1, 2], [2, 16]], 0, 32), (), ["small0"])
+    op("g", lambda: g.iota(T.small[:, 32:64], [[-1, 32]], 32, 1), (), ["small1"])
     ms(T.one[:, :], 1.0, ["one"])
+    ms(T.comb[:, :], 0.0, ["comb"])
     ms(T.lraw[:, :], math.log(2.0), ["lraw"])
-    ms(T.rp[:, :], 0.0, ["rp"])
-    ms(T.vn[:, :], -1.0 / 256, ["vn"])
-    ms(T.vz[:, :], 2.0 / 256, ["vz"])
-    for j in range(4):
-        ms(T.wm[32 * j:32 * (j + 1), :], 2.0 ** (j - 1) / 32, ["wm%d" % j])
-    ms(T.rp[:, 15:144:16], 2.0, ["rp"])
-    cp(T.msg0[:, :], T.kin_i[:, :], ["kin"], ["msg0"])
-    send(0)
+    ms(T.comb[:, 15:144:16], 2.0, ["comb"])
     asel(T.id32[:, :], [[-1, 128]], A.is_equal, 0.0, 0, 1, "id32", T.one[:, :], "one")
-    asel(T.rp[:, :], [[-1, 144]], A.is_ge, 0.0, 15, 1, "rp")
+    asel(T.rp[:, :], [[-1, 144]], A.is_ge, 0.0, 15, 1, "rp", T.comb[:, :], "comb")
     asel(T.rp[:, :], [[1, 144]], A.is_ge, 0.0, 0, -1, "rp")
-    op("g", lambda: g.iota(T.a16[:, :], [[16, P]], 16 * P * r, 0, allow_small_or_imprecise_dtypes=True), (), ["a16"])
+    ms(T.ones[:, :], 1.0, ["ones"])
+    ms(plane(T.qm, 4), 3072.0, ["qm4"])
+    for j in range(4):
+        ms(plane(T.qc, j), 192.0 * 2 ** j, ["qc%d" % j])
+        ms(T.wm[32 * j:32 * (j + 1), :], 2.0 ** j / 32, ["wm%d" % j])
+    ts(T.small[:, 64:96], T.small[:, 0:32], P - 1, None, A.bitwise_and, None, ["small0"], ["small2"])
+    ts(T.small[:, 96:128], T.small[:, 32:64], 15, None, A.bitwise_and, None, ["small1"], ["small3"])
+    cp(T.turn[:, :], T.small[:, 64:96], ["small2"], ["turn"])
+    ts(T.k16[:, :], T.small[:, 96:128], 0.0, 1 / 16, A.is_equal, A.mult, ["small3"], ["k16"])
+    cp(T.msg0[:, :], T.kin_i[:, :], ["kin"], ["msg0"])
+    send(0, ["msg0"])
+    op("g", lambda: g.iota(T.a32[:, :], [[16, P]], 16 * (P * r - 2048), 0, allow_small_or_imprecise_dtypes=True), (), ["a32"])
     asel(T.lraw[:, :], [[1, 128]], A.is_gt, -math.log(32.0), 0, -1, "lraw")
     asel(T.lraw[:, :], [[1, 128]], A.not_equal, -200.0, 0, -1, "lraw")
     asel(T.lraw[:, :], [[-16, 8], [0, 16]], A.is_ge, -200.0, 0, 1, "lraw")
     asel(T.lraw[:, :], [[16, 8], [0, 16]], A.is_ge, -200.0, 15, -1, "lraw")
+    ts(T.tab[:, r * P:(r + 1) * P], T.msg0[:, :], -SHIFT, None, A.add, None, ["msg0"], allown)
+    ts(T.idh[:, :], T.id32[:, :], -1.0, None, A.mult, None, ["id32"], ["idh"])
+    for i, x in enumerate(IDB):
+        ts(T.idb[:, 128 * i:128 * (i + 1)], T.id32[:, :], x, None, A.mult, None, ["id32"], ["idb%d" % i])
+    op("p", None, ["idb%d" % i for i in range(len(IDB))])
+    for step in offsets(0):
+        step()
+    prepare(0)
     act(T.tri[:, :], T.lraw[:, :], F.Exp, 0.0, 1.0, ["lraw"], ["tri"])
-    prep_first(0)
-    take(0, r)
-    prep_rest(0)
     for t in range(RO):
         q0 = 17 * t + 3
         ts(T.sel[:, 128 * t:128 * (t + 1)], T.one[:, :], T.id32[:, q0:q0 + 1], None, A.mult, None, ["one", "id32"], ["sel%d" % t])
-    for i, x in enumerate(IDS):
-        ts(T.ids[:, 128 * i:128 * (i + 1)], T.id32[:, :], x, None, A.mult, None, ["id32"], ["ids"])
+    ts(T.vt[:, :], T.id32[:, :], -1.0, 2.0, A.mult, A.add, ["id32"], ["vt"])
+    ts(T.vz[:, :], T.id32[:, :], 2.0, -4.0, A.mult, A.add, ["id32"], ["vz"])
+    ts(T.vk[:, :], T.id32[:, :], 0.5, -1 / 256, A.mult, A.add, ["id32"], ["vk"])
     for s in senders:
         take(0, s)
+        if s == senders[1]:
+            cp(T.a16[:, :], T.a32[:, :], ["a32"], ["a16"])
 
-    H, G = C, 16 * C
     for t in range(RO):
         par = t % 2
         last = t == RO - 1
+        sel, seltok = T.sel[:, 128 * t:128 * (t + 1)], "sel%d" % t
 
         def gather(e, lo, hi):
-            src = T.tab[:, :].indirect(T.off[:, lo:hi])
-            out = T.gat[:, 16 * lo:16 * hi]
-            toks = ["gat%d" % i for i in range(lo // 8, hi // 8)]
+            src, out = T.tab[:, :].indirect(T.off[:, 8 * lo:8 * hi]), T.gat[:, H * lo:H * hi]
+            toks = ["gat%d" % i for i in range(lo, hi)]
             if e == "v":
                 cp(out, src, alltab + ["off"], toks)
             else:
                 act(out, src, F.Identity, 0.0, 1.0, alltab + ["off"], toks)
 
-        def gtok(c):
-            return ["gat%d" % i for i in range(16 * c, 16 * c + 16)]
-
-        def braw(c):
-            b = "bc"[c % 2]
-            mm(T["ps" + b][:, E - H:E], T.sel[:, 128 * t:128 * (t + 1)], T.gat[:, G * c + t:G * (c + 1):16], True, True,
-               gtok(c) + ["sel%d" % t], ["W%s0_0" % b], [b])
-
-        def bmake(c):
-            b = "bc"[c % 2]
-            ts(T.psh[:, c * H:(c + 1) * H], T["ps" + b][:, E - H:E], MAGIC, MAGIC, A.add, A.subtract, ["W%s0_0" % b], ["B%d" % c], [b, "h"])
-
-        def emake(c):
-            tt(T.e16[:, c * H:(c + 1) * H], T.psh[:, c * H:(c + 1) * H], T.n16[:, c * H:(c + 1) * H], A.subtract,
-               ["B%d" % c, "n16"], ["e16_%d" % c], ["h"])
-
-        def subs(c, kq, ks=range(4)):
-            for k in [4 * kq + i for i in ks]:
-                o = G * c + H * k
-                tt(T.dif[:, o:o + H], T.gat[:, G * c + k:G * (c + 1):16], T.psh[:, c * H:(c + 1) * H], A.subtract,
-                   gtok(c) + ["B%d" % c], ["d%d_%d" % (c, k)], ["h"])
-
-        def clamp(c, kq):
-            o = G * c + 4 * H * kq
-            toks = ["d%d_%d" % (c, k) for k in range(4 * kq, 4 * kq + 4)]
-            ts(T.dif[:, o:o + 4 * H], T.dif[:, o:o + 4 * H], -8.0, 8.0, A.max, A.min, toks, toks)
-
-        def sclamp(c, kq):
-            o = G * c + 4 * H * kq
-            toks = ["d%d_%d" % (c, k) for k in range(4 * kq, 4 * kq + 4)]
-            sl = slice(c * H, (c + 1) * H)
-            act(T.eabs[:, sl], T.e16[:, sl], F.Abs, 0.0, 1.0, ["e16_%d" % c], ["eabs%d" % c])
-            act(T.dif[:, o:o + 4 * H], T.dif[:, o:o + 4 * H], F.Relu, 8.0, -1.0, toks, toks)
-            act(T.nown[:, sl], T.eabs[:, sl], F.Sign, -8.0, 1.0, ["eabs%d" % c], ["nown%d" % c])
-            act(T.dif[:, o:o + 4 * H], T.dif[:, o:o + 4 * H], F.Relu, 16.0, -1.0, toks, toks)
-            act(T.mul[:, sl], T.nown[:, sl], F.Identity, (1 + 1 / 4096) / 2, (1 - 1 / 4096) / 2, ["nown%d" % c], ["mul%d" % c])
-
-        def clamp2(c, k, sp=False):
-            o = G * c + H * k
-            toks = ["d%d_%d" % (c, k), "d%d_%d" % (c, k + 1)]
-            ts(T.dif[:, o:o + 2 * H], T.dif[:, o:o + 2 * H], -8.0, 8.0, A.max, A.min, toks, toks)
+        def name():
+            ts(T.gb[:, :], plane(T.gat, 0), MAGIC, MAGIC, A.add, A.subtract, ["gat0", "gat1"], ["gb"])
             for i in range(2):
-                mm(T.psa[:, c * H:(c + 1) * H], T.rp[:, 15 - k - i:143 - k - i], T.dif[:, o + i * H:o + (i + 1) * H], False,
-                   sp and i == 1, [toks[i], "rp"], ["P%d" % c], ["a"])
+                mm(NAME, i * E, (i + 1) * E, sel, T.gb[:, :], True, True, [seltok, "gb"])
+            mm(CODE, 0, E, idb(-1.0), T.ones[:, :], True, False, ["ones"])
 
-        def elect():
-            for c in range(2):
-                tt(T.pi[:, c * H:(c + 1) * H], T.psa[:, c * H:(c + 1) * H], T.mul[:, c * H:(c + 1) * H], A.mult,
-                   ["P%d" % c, "mul%d" % c], ["pi0" if c else "pia"], ["a"])
-            for c in range(2):
-                ts(T.uu[:, 2 * E + c * H:2 * E + (c + 1) * H], T.pi[:, c * H:(c + 1) * H], 1 + (2 << 2), None, A.bitwise_and, None,
-                   ["pi0" if c else "pia"], ["u0_2" if c else "ua"])
-            umake(0, 3)
-            umake(0, 0)
-            ts(col(T.tes, 0), col(T.uu, 0, 2), 0.0, 2.0, A.is_gt, A.subtract, ["u0_2"], ["tes0"])
-            vote(0, 2, 0)
-            zmake(0, 2)
-            vote(0, 2, 1)
-            vote(0, 3, 0)
-            umake(0, 1)
-            zmake(0, 3)
-            vote(0, 3, 1)
-            vote(0, 0, 0)
-            zmake(0, 0)
-            vote(0, 0, 1)
-            vote(0, 1, 0)
-            zmake(0, 1)
-            vote(0, 1, 1)
-            key(0, 40.0, T.tes, 0, ["tes0"])
-            gmake(0, 2)
-            gmake(0, 3)
-            for j in (2, 3, 0, 1):
-                key(0, -1.0, T.zz, j, ["z0_%d" % j])
-            sign(0, 2)
-            sign(0, 3)
-            gmake(0, 0)
-            gmake(0, 1)
-            for j in (2, 3, 0, 1):
-                key(0, 2.0, T.gg, j, ["g0_%d" % j], sp=j == 1)
-            sign(0, 0)
-            act(col(T.xx, 0), col(T.psd, 0), F.Exp, 44.5 * LN64, LN64, ["key0"], ["xx"], ["d"])
-            sign(0, 1)
-            mm(col(T.psa, 0), T.tri[:, :], col(T.xx, 0), True, True, ["tri", "xx"], ["P0", "P1"], ["a"])
-            mm(col(T.pse, 0), T.wm[:, :], col(T.om, 0), False, True,
-               ["wm%d" % j for j in range(4)] + ["om0_%d" % j for j in range(4)], ["delta0"], ["e"])
-            if not last:
-                prep_first(t + 1)
-            hv = [slice(0, H), slice(H, E)]
-            for c in range(2):
-                tt(T.win[:, hv[c]], T.psa[:, hv[c]], T.xx[:, hv[c]], A.is_lt, ["P%d" % c, "xx"], ["win%d" % c], ["a"])
-            for c in range(2):
-                tt(T.psh[:, E + c * H:E + (c + 1) * H], T.pse[:, hv[c]], T.win[:, hv[c]], A.mult, ["delta0", "win%d" % c], ["tt%d" % c],
-                   ["e", "h"])
-            for c in range(2):
-                o = r * P + 2 * c * H
-                tt(T.ss[:, hv[c]], T.psh[:, E + c * H:E + (c + 1) * H], T.tab[:, o + par:o + 2 * H:2], A.add,
-                   ["tt%d" % c, tabtok(r, par, c)], ["ss%d" % c], ["h"])
-            for c in range(2):
-                if last:
-                    ts(T.yo[:, 2 * c * H + par:2 * (c + 1) * H:2], T.ss[:, hv[c]], 7.5, None, A.add, None, ["ss%d" % c], ["yo%d" % c])
-                else:
-                    ts(T["msg%d" % (t + 1)][:, hv[c]], T.ss[:, hv[c]], 7.5, None, A.add, None, ["ss%d" % c],
-                       ["msg%s%d" % ("a" if c == 0 else "", t + 1)])
-            if last:
-                op("y", lambda: g.sync.dma_start(T.yk[:, :], T.yo[:, :]).then_inc(T.sem.stored, 16),
-                   ["yo0", "yo1", "yo2"], ["yk1"], (), ("stored", 16))
-            else:
-                send(t + 1)
+        def sub(k, n):
+            tt(plane(T.dif, k, n), plane(T.gat, k, n), ps(NAME, 0, n * E), A.subtract,
+               ["gat%d" % i for i in range(2 * k, 2 * (k + n))] + ["ps" + NAME], ["dif%d" % i for i in range(k, k + n)], [NAME])
 
-        def compare():
-            gather("v", 0, 64)
-            gather("s", 64, 128)
-            gather("v", 128, 152)
-            gather("s", 160, 256)
-            braw(0)
-            bmake(0)
-            gather("v", 152, 160)
-            subs(0, 0)
-            emake(0)
-            subs(0, 1)
-            clamp(0, 0)
-            reduce4(0, 0, st=True)
-            braw(1)
-            subs(0, 2)
-            clamp(0, 1)
-            reduce4(0, 1)
-            sclamp(0, 2)
-            subs(0, 3)
-            bmake(1)
-            clamp(0, 3)
-            emake(1)
-            subs(1, 0)
-            reduce4(0, 3)
-            ownadd(0)
-            reduce4(0, 2, sp=True)
-            sclamp(1, 0)
-            delta(0)
-            subs(1, 1)
-            subs(1, 2)
-            clamp(1, 1)
-            reduce4(1, 1, st=True)
-            key(0, -4.5, T.nown, 0, ["nown0", "nown1"], st=True)
-            ownadd(1)
-            subs(1, 3, [0, 1])
-            clamp(1, 2)
-            reduce4(1, 2)
-            reduce4(1, 0)
-            subs(1, 3, [2, 3])
-            clamp2(1, 12)
-            clamp2(1, 14, sp=True)
-            skipmake(0)
+        def clamp(k, n):
+            toks = ["dif%d" % i for i in range(k, k + n)]
+            ts(plane(T.dif, k, n), plane(T.dif, k, n), -8.0, 8.0, A.max, A.min, toks, toks)
+            for i in range(k, k + n):
+                row = (t + i) % 16
+                mm(CODE, 0, E, T.rp[:, 15 - row:143 - row], plane(T.dif, i), False, i == 15, ["dif%d" % i, "rp"])
 
-        def reduce4(c, kq, st=False, sp=False):
-            for k in range(4 * kq, 4 * kq + 4):
-                o = G * c + H * k
-                mm(T.psa[:, c * H:(c + 1) * H], T.rp[:, 15 - k:143 - k], T.dif[:, o:o + H], st and k % 4 == 0, sp and k % 4 == 3,
-                   ["d%d_%d" % (c, k), "rp"], ["P%d" % c], ["a"])
+        def half(buf, c, j=0):
+            return buf[:, j * E + c * H:j * E + (c + 1) * H]
 
-        def ownadd(c):
-            mm(T.psa[:, c * H:(c + 1) * H], ident(-5120.0), T.nown[:, c * H:(c + 1) * H], False, False,
-               ["nown%d" % c, "ids"], ["P%d" % c], ["a"])
+        def named(bank, lo, other, tok, sp=True):
+            mm(bank, lo, lo + E, sel, T.gb[:, :], True, False, [seltok, "gb"])
+            mm(bank, lo, lo + E, T.idh[:, :], other, False, sp, ["idh", tok])
 
-        def key(c, x, buf, j, toks, st=False, sp=False):
-            mm(col(T.psd, c), ident(x), col(buf, c, j), st, sp, toks + ["ids"], ["key%d" % c], ["d"])
+        def selves():
+            named(SELF, 0, T.n16[:, :], "n16")
+            named(SELF, E, T.a16[:, par:P:2], "a16")
 
-        def col(buf, c, j=0):
-            return buf[:, j * E + PIECE[c][0]:j * E + PIECE[c][1]]
+        def not_own():
+            ts(plane(T.no, 0), ps(SELF, 0, E), 0.0, None, A.not_equal, None, ["ps" + SELF], ["no"], [SELF])
 
-        def each(name, c):
-            return ["%s%d" % (name, q) for q in CHUNKS[c]]
+        def not_skipped():
+            act(plane(T.sg, 0), ps(SELF, E, 2 * E), F.Sign, 0.0, 1.0, ["ps" + SELF], ["sg"], [SELF])
+            act(plane(T.no, 1), plane(T.sg, 0), F.Abs, 0.0, 1.0, ["sg"], ["noskip"])
 
-        def wreg(c, j):
-            b = "bc"[j // 2]
-            return col(T["ps" + b], c, j % 2), "W%s%d_%d" % (b, j % 2, c), b
+        def code(c):
+            tt(half(T.pi, c), ps(CODE, c * H, (c + 1) * H), half(T.no, c), A.mult, ["ps" + CODE, "no"], ["pi%d" % c], [CODE])
 
-        def delta(c):
-            mm(col(T.pse, c), T.id32[:, :], col(T.e16, c), True, False, ["id32"] + each("e16_", c), ["delta%d" % c], ["e"])
-            mm(col(T.pse, c), ident(-1.0), col(T.ma, c), False, False, ["ids", "ma"], ["delta%d" % c], ["e"])
+        def bit(j, c=None):
+            out, src = (plane(T.uu, j), T.pi[:, :]) if c is None else (half(T.uu, c, j), half(T.pi, c))
+            cs = [0, 1] if c is None else [c]
+            ts(out, src, 1 + (2 << j), None, A.bitwise_and, None, ["pi%d" % x for x in cs], ["u%d_%d" % (x, j) for x in cs])
 
-        def skipmake(c):
-            tt(col(T.skip, c), col(T.psh, c), T.a16[:, 2 * PIECE[c][0] + par:2 * PIECE[c][1]:2], A.is_equal, each("B", c) + ["a16"],
-               ["skip%d" % c], ["h"])
-            key(c, -60.0, T.skip, 0, ["skip%d" % c])
+        def speaks(j):
+            ts(T.tes[:, :], plane(T.uu, j), (2 << j) + 0.5, None, A.is_lt, None, ["u0_%d" % j, "u1_%d" % j], ["tes"])
 
-        def umake(c, j):
-            ts(col(T.uu, c, j), col(T.pi, c), 1 + (2 << j), None, A.bitwise_and, None, ["pi%d" % c], ["u%d_%d" % (c, j)])
+        def same(j):
+            b = MINE[j // 2]
+            tt(plane(T.zz, j), plane(T.uu, j), ps(b, j % 2 * E, (j % 2 + 1) * E), A.is_equal,
+               ["u0_%d" % j, "u1_%d" % j, "ps" + b], ["z%d" % j], [b])
 
-        def zmake(c, j):
-            b = "fg"[j // 2]
-            tt(col(T.zz, c, j), col(T.uu, c, j), col(T["ps" + b], c, j % 2), A.is_equal,
-               ["u%d_%d" % (c, j), "A" + b], ["z%d_%d" % (c, j)], [b])
+        def vote(j):
+            mm(VOTE[j], 0, E, T.vt[:, :], T.tes[:, :], True, False, ["vt", "tes"])
 
-        def vote(c, j, part):
-            w, tok, b = wreg(c, j)
-            if part == 0:
-                mm(w, T.vn[:, :], col(T.tes, c), True, False, ["vn", "tes%d" % c], [tok], [b])
-            else:
-                mm(w, T.vz[:, :], col(T.zz, c, j), False, True, ["vz", "z%d_%d" % (c, j)], [tok], [b])
+        def vote_same(j):
+            mm(VOTE[j], 0, E, T.vz[:, :], plane(T.zz, j), False, True, ["vz", "z%d" % j])
 
-        def sign(c, j):
-            w, tok, b = wreg(c, j)
-            lo, hi = PIECE[c]
-            o = (j % 2) * E
-            act(T.om[32 * j:32 * (j + 1), lo:hi], T["ps" + b][32 * j:32 * (j + 1), o + lo:o + hi], F.Sign, 1 - 1 / 512, -1.0,
-                [tok], ["om%d_%d" % (c, j)], [b])
+        def against(j):
+            act(plane(T.gg, j), ps(VOTE[j], 0, E), F.Abs, -1.0, 1.0, ["ps" + VOTE[j]], ["g%d" % j], [VOTE[j]])
 
-        def gmake(c, j):
-            w, tok, b = wreg(c, j)
-            tt(col(T.gg, c, j), col(T.zz, c, j), w, A.is_gt, ["z%d_%d" % (c, j), tok], ["g%d_%d" % (c, j)], [b])
+        def key_begin():
+            mm(KEY, 0, E, idb(-9.0), plane(T.no, 0), True, False, ["no"])
+            mm(KEY, 0, E, idb(60.0), plane(T.no, 1), False, False, ["noskip"])
 
-        compare()
+        def key_silent():
+            mm(KEY, 0, E, idb(40.0), T.tes[:, :], False, False, ["tes"])
+
+        def key(j):
+            mm(KEY, 0, E, T.vk[:, :], plane(T.gg, j), False, j == 3, ["vk", "g%d" % j])
+
+        def elected(j):
+            b = VOTE[j]
+            tt(T.om[32 * j:32 * (j + 1), :], T["ps" + b][32 * j:32 * (j + 1), 0:E], T.zz[32 * j:32 * (j + 1), j * E:(j + 1) * E],
+               A.is_gt, ["ps" + b, "z%d" % j], ["om%d" % j], [b])
+
+        def change_begin():
+            named(DELTA, 0, T.n16[:, :], "n16", False)
+            mm(DELTA, 0, E, idb(-1.0), T.ma[:, :], False, False, ["ma"])
+
+        def change():
+            mm(DELTA, 0, E, T.wm[:, :], T.om[:, :], False, True, ["wm%d" % j for j in range(4)] + ["om%d" % j for j in range(4)])
+
+        def power():
+            act(T.xx[:, :], ps(KEY, 0, E), F.Exp, -91.0 * LN64, LN64, ["ps" + KEY], ["xx"], [KEY])
+
+        def rivals():
+            mm(RIVAL, 0, E, T.tri[:, :], T.xx[:, :], True, True, ["tri", "xx"])
+
+        def first(c):
+            tt(half(T.win, c), ps(RIVAL, c * H, (c + 1) * H), half(T.xx, c), A.is_lt, ["ps" + RIVAL, "xx"], ["win%d" % c], [RIVAL])
+
+        def apply(c):
+            tt(ps(DELTA, E + c * H, E + (c + 1) * H), ps(DELTA, c * H, (c + 1) * H), half(T.win, c), A.mult,
+               ["ps" + DELTA, "win%d" % c], ["tt%d" % c], [DELTA])
+
+        def update(c):
+            o = own(par, c * H, (c + 1) * H)
+            tt(o, ps(DELTA, E + c * H, E + (c + 1) * H), o, A.add, ["tt%d" % c, owntok(par, c)], [owntok(par, c)], [DELTA])
+
+        def pack(c):
+            lo, hi = c * H, (c + 1) * H
+            out = T.yo[:, 2 * lo + par:2 * hi:2] if last else T["msg%d" % (t + 1)][:, lo:hi]
+            ts(out, own(par, lo, hi), SHIFT, None, A.add, None, [owntok(par, c)], ["new%d" % c])
+
+        gather("v", *BY_VECTOR[0])
+        gather("v", *BY_VECTOR[1])
+        name()
+        gather("v", *BY_VECTOR[2])
+        for lo, hi in BY_SCALAR:
+            gather("s", lo, hi)
+        selves(); change_begin(); sub(0, 2)
+        for k in range(2, 14, 2):
+            sub(k, 2); clamp(k - 2, 2)
+        sub(14, 1); clamp(12, 2); sub(15, 1); clamp(14, 1); clamp(15, 1)
+        nxt = offsets(t + 1) if not last else [lambda: None] * 10
+        not_own(); not_skipped()
+        code(0); code(1); key_begin(); bit(0, 0); bit(0, 1); bit(1); speaks(0); same(0); vote(0); vote_same(0); against(0); vote(1); bit(2)
+        same(1); vote_same(1); against(1); vote(2); bit(3); same(2); vote_same(2); against(2); vote(3); key_silent()
+        same(3); vote_same(3); against(3); key(0); key(1); key(2); key(3); power(); rivals()
+        elected(0); elected(1); elected(2); elected(3); change(); nxt[0]()
+        first(0); first(1); apply(0); apply(1); update(0); update(1); pack(0); pack(1)
         if last:
-            act(T.yo[:, 1 - par:P:2], T.tab[:, r * P + 1 - par:(r + 1) * P:2], F.Identity, 7.5, 1.0,
-                [tabtok(r, 1 - par, 0), tabtok(r, 1 - par, 1)], ["yo2"])
-        elect()
-        if not last:
-            take(t + 1, r)
-            prep_rest(t + 1)
+            act(T.yo[:, 1 - par:P:2], own(1 - par), F.Identity, SHIFT, 1.0, [owntok(1 - par, 0), owntok(1 - par, 1)], ["kept"])
+            op("y", lambda: g.sync.dma_start(T.yk[:, :], T.yo[:, :]).then_inc(T.sem.stored, 16),
+               ["new0", "new1", "kept"], ["yk1"], (), ("stored", 16))
+        else:
+            send(t + 1, ["new0", "new1"])
+            for step in nxt[1:-1]:
+                step()
+            prepare(t + 1)
             for s in senders:
                 take(t + 1, s)
+                if s == senders[0]:
+                    nxt[-1]()
     op("y", None, ["yk1"], ())
-    op("g", None, ["out%d" % (len(MSGS) - 1)], ())
+    op("g", None, ["out%d" % (RO - 1)], ())
     emit(g, T, ops)

import math
from concourse.bass import DstId, RemoteDMATransfer
from concourse.mybir import AluOpType as A, ActivationFunctionType as F

N, P, E, RO = 8, 512, 256, 5
MAGIC = 201326592.0
LN64 = math.log(64.0)
SHIFT = 32775.5
H = 128
BY_SCALAR = [(6, 8), (8, 12), (12, 16), (16, 20), (20, 24), (24, 28), (28, 30), (30, 32)]
BY_VECTOR = [(0, 2), (2, 4), (4, 6)]
IDB = [-1.0, 2.0, -2.0, -9.0, 60.0, 40.0]

SCRATCH = {
    "kin_i": ("sbuf", [128, P], "int32"),
    "msg0": ("sbuf", [128, P], "uint16"),
    "land0": ("sbuf", [128, N * P], "uint16"),
    "tab": ("sbuf", [128, N * P], "float32"),
    "gat": ("sbuf", [128, 16 * E], "float32"),
    "dif": ("sbuf", [128, 16 * E], "bfloat16"),
    "off": ("sbuf", [128, E], "uint16"),
    "turn": ("sbuf", [128, 32], "uint16"),
    "small": ("sbuf", [128, 128], "int32"),
    "k16": ("sbuf", [128, 32], "float16"),
    "nt": ("sbuf", [128, E], "float16"),
    "nx": ("sbuf", [128, 8 * E], "float16"),
    "gb": ("sbuf", [128, E], "float16"),
    "n16": ("sbuf", [128, E], "float16"),
    "a16": ("sbuf", [128, P], "float16"),
    "ma": ("sbuf", [128, E], "bfloat16"),
    "qm": ("sbuf", [128, 5 * E], "bfloat16"),
    "qc": ("sbuf", [128, 4 * E], "bfloat16"),
    "sg": ("sbuf", [128, 2 * E], "bfloat16"),
    "no": ("sbuf", [128, 2 * E], "bfloat16"),
    "pi": ("sbuf", [128, E], "int32"),
    "uu": ("sbuf", [128, 4 * E], "int32"),
    "tes": ("sbuf", [128, E], "bfloat16"),
    "zz": ("sbuf", [128, 4 * E], "bfloat16"),
    "gg": ("sbuf", [128, 4 * E], "bfloat16"),
    "om": ("sbuf", [128, E], "bfloat16"),
    "xx": ("sbuf", [128, E], "bfloat16"),
    "win": ("sbuf", [128, E], "bfloat16"),
    "yo": ("sbuf", [128, P], "float32"),
    "a32": ("sbuf", [128, P], "float32"),
    "one": ("sbuf", [128, 128], "float32"),
    "ones": ("sbuf", [128, E], "bfloat16"),
    "id32": ("sbuf", [128, 128], "float32"),
    "idb": ("sbuf", [128, 128 * len(IDB)], "bfloat16"),
    "idh": ("sbuf", [128, 128], "float16"),
    "sel": ("sbuf", [128, 128 * RO], "float16"),
    "comb": ("sbuf", [128, 144], "bfloat16"),
    "rp": ("sbuf", [128, 144], "bfloat16"),
    "lraw": ("sbuf", [128, 128], "float32"),
    "tri": ("sbuf", [128, 128], "bfloat16"),
    "vt": ("sbuf", [128, 128], "bfloat16"),
    "vz": ("sbuf", [128, 128], "bfloat16"),
    "vk": ("sbuf", [128, 128], "bfloat16"),
    "wm": ("sbuf", [128, 128], "bfloat16"),
}
for _t in range(1, RO):
    SCRATCH["msg%d" % _t] = ("sbuf", [128, E], "uint16")
    SCRATCH["land%d" % _t] = ("sbuf", [128, N * E], "uint16")
for _b in "abcdefgh":
    SCRATCH["ps" + _b] = ("psum", [128, 512], "float32")

NAME = "a"
CODE = "c"
RIVAL = "c"
KEY = "d"
DELTA = "e"
MINE = "fg"
SELF = "h"
VOTE = "abhf"

SEMAPHORES = (["sv", "ss", "sp", "sg", "loaded", "stored", "sent"] + ["rin%d" % m for m in range(RO)]
              + ["arr%d_%d" % (m, r) for m in range(RO) for r in range(N)])


def bits(engs):
    m = 0
    for e in engs:
        m |= 1 << e
    return m


def routes(T, topo):
    cores = list(T.cores)
    out = []
    for r, c in enumerate(cores):
        near = [s for s in range(N) if s != r and topo.may_write(c, cores[s])]
        far = [s for s in range(N) if s != r and s not in near]
        able = [h for h in topo.cores_of(c) if h != c and all(topo.may_write(h, cores[s]) for s in far)]
        able.sort(key=lambda h: topo.die(h) == topo.die(c))
        i = sorted(near + [r]).index(r)
        far = far[i % len(far):] + far[:i % len(far)]
        near = [s for s in near if s > r] + [s for s in near if s < r]
        out.append((near, {able[0]: far[0::2], able[1]: far[1::2]}))
    return out


def one_to_many(g, T, topo, src_core, dst_cores, src, dst, sem, engs):
    ids = []
    for d in dst_cores:
        rid, pid = topo.addr(d, src_core)
        ids.append(DstId(rid=rid, pnc=pid))
    return RemoteDMATransfer(dst_ids=ids, dma_engine_mask=bits(engs), remote_sem=sem, srcs=[src], dsts=[dst] * len(ids))


def width(x):
    return P if x == 0 else E


def helper_program(g, core, T, topo, r, dsts):
    cores = list(T.cores)
    n_in = len(topo.engines(cores[r], core)) // 2
    engs = topo.engines(core, cores[dsts[0]])
    for m in range(RO):
        n = width(m)
        g.wait_ge(T.sem["rin%d" % m], n_in)
        tr = one_to_many(g, T, topo, core, [cores[s] for s in dsts], T["msg%d" % m][:, :],
                         T["land%d" % m][:, r * n:(r + 1) * n], T.sem["arr%d_%d" % (m, r)], engs)
        g.remote_dma_fused([tr], local_sem=T.sem.sent)
    g.wait_ge(T.sem.sent, RO * len(engs))


def emit(g, T, ops):
    q = {"v": g.vector, "s": g.scalar, "p": g.tensor, "g": g, "y": g.sync}
    semname = {"v": "sv", "s": "ss", "p": "sp", "g": "sg"}
    lastw, readers, bank = {}, {}, {}
    deps = []
    for i, (e, fn, rd, wr, bk, ev) in enumerate(ops):
        d = set()
        for k in rd:
            if k in lastw:
                d.add(lastw[k])
        for k in wr:
            if k in lastw:
                d.add(lastw[k])
            d.update(readers.get(k, []))
        for k in bk:
            for e2, j in bank.get(k, {}).items():
                if e2 != e:
                    d.add(j)
        d.discard(i)
        if e == "p":
            d = set(j for j in d if ops[j][0] != "p")
        best = {}
        keep = set()
        for j in d:
            if ops[j][5] is not None:
                keep.add(j)
            else:
                best[ops[j][0]] = max(best.get(ops[j][0], -1), j)
        keep.update(best.values())
        deps.append(keep)
        for k in rd:
            readers.setdefault(k, []).append(i)
        for k in wr:
            lastw[k] = i
            readers[k] = []
        for k in bk:
            bank.setdefault(k, {})[e] = i
    seen = {}
    for i, op in enumerate(ops):
        keep = set()
        for j in deps[i]:
            if ops[j][5] is not None:
                key, val = (op[0], ops[j][5][0]), ops[j][5][1]
            else:
                key, val = (op[0], ops[j][0]), j
            if seen.get(key, -1) < val:
                seen[key] = val
                keep.add(j)
        deps[i] = keep
    need = set()
    for d in deps:
        need.update(d)
    count = {"v": 0, "s": 0, "p": 0, "g": 0}
    event = {}
    for i, (e, fn, rd, wr, bk, ev) in enumerate(ops):
        for j in sorted(deps[i]):
            q[e].wait_ge(T.sem[event[j][0]], event[j][1])
        ins = fn() if fn is not None else None
        if ev is not None:
            event[i] = ev
        elif i in need:
            count[e] += 1
            ins.then_inc(T.sem[semname[e]], 1)
            event[i] = (semname[e], count[e])


def rank_program(g, core, T, topo):
    cores = list(T.cores)
    plan = routes(T, topo)
    r = T.rank_of(core)
    if r is None:
        for s in range(N):
            if core in plan[s][1]:
                helper_program(g, core, T, topo, s, plan[s][1][core])
        return
    near, helpers = plan[r]
    from_near = sorted(near, key=lambda s: plan[s][0].index(r))
    from_far = sorted([s for s in range(N) if s != r and s not in near],
                      key=lambda s: [d.index(r) for d in plan[s][1].values() if r in d][0])
    senders = from_near[:2] + from_far[:2] + from_near[2:] + from_far[2:]
    hs = list(helpers.keys())
    V, S, PE = g.vector, g.scalar, g.tensor
    ops = []

    def op(e, fn, rd=(), wr=(), bk=(), ev=None):
        ops.append((e, fn, list(rd), list(wr), list(bk), ev))

    def ts(out, in0, s1, s2, o0, o1, rd, wr, bk=()):
        if o1 is None:
            op("v", lambda: V.tensor_scalar(out, in0, s1, None, o0), rd, wr, bk)
        else:
            op("v", lambda: V.tensor_scalar(out, in0, s1, s2, o0, o1), rd, wr, bk)

    def tt(out, in0, in1, o, rd, wr, bk=()):
        op("v", lambda: V.tensor_tensor(out, in0, in1, o), rd, wr, bk)

    def cp(out, in_, rd, wr, bk=()):
        op("v", lambda: V.tensor_copy(out, in_), rd, wr, bk)

    def ms(ap, val, wr):
        op("v", lambda: V.memset(ap, val), (), wr)

    def act(out, in_, f, bias, scale, rd, wr, bk=()):
        op("s", lambda: S.activation(out, in_, f, bias=bias, scale=scale), rd, wr, bk)

    def mm(bank, lo, hi, lhsT, rhs, st, sp, rd, step=1):
        out = T["ps" + bank][:, lo:hi] if step == 1 else T["ps" + bank][:, lo:hi:step]
        op("p", lambda: PE.matmul(out, lhsT, rhs, st, sp), rd, ["ps" + bank], [bank])

    def asel(ap, pat, cmp, fill, base, cm, tok, src=None, srctok=None):
        op("g", lambda: g.affine_select(ap, ap if src is None else src, pat, cmp, fill, base, cm),
           [tok if srctok is None else srctok], [tok])

    def idb(x):
        i = IDB.index(x)
        return T.idb[:, 128 * i:128 * (i + 1)]

    def ps(bank, lo, hi):
        return T["ps" + bank][:, lo:hi]

    sent = [0]

    def send(m, toks):
        n = width(m)
        src = T["msg%d" % m][:, :]
        on = topo.engines(core, hs[0])
        h = len(on) // 2
        trs = [one_to_many(g, T, topo, core, [hs[i]], src, src, T.sem["rin%d" % m], on[i * h:(i + 1) * h]) for i in range(2)]
        offc = topo.engines(core, cores[near[0]])
        tr = one_to_many(g, T, topo, core, [cores[s] for s in near], src, T["land%d" % m][:, r * n:(r + 1) * n],
                         T.sem["arr%d_%d" % (m, r)], offc)
        sent[0] += len(on) + len(offc)

        def go():
            g.remote_dma_fused(trs, local_sem=T.sem.sent)
            g.remote_dma_fused([tr], local_sem=T.sem.sent)
        op("g", go, toks, ["out%d" % m], (), ("sent", sent[0]))

    def owntok(par, c):
        return "own%d_%d" % (par, c)
    allown = [owntok(par, c) for par in range(2) for c in range(2)]
    alltab = ["tab%d" % s for s in range(N) if s != r] + allown

    def own(par, lo=0, hi=E):
        return T.tab[:, r * P + 2 * lo + par:r * P + 2 * hi:2]

    def plane(buf, i, k=1):
        return buf[:, i * E:(i + k) * E]

    def take(m, s):
        n = width(m)
        tok = "land%d_%d" % (m, s)
        op("x", None, (), [tok], (), ("arr%d_%d" % (m, s), len(topo.engines(cores[s], cores[plan[s][0][0]]))))
        out = T.tab[:, s * P:(s + 1) * P] if m == 0 else T.tab[:, s * P + (m - 1) % 2:(s + 1) * P:2]
        ts(out, T["land%d" % m][:, s * n:(s + 1) * n], -SHIFT, None, A.add, None, [tok], ["tab%d" % s])

    def offsets(t):
        src = T.tab[:, r * P:(r + 1) * P].indirect(T.turn[:, 16 * (t % 2):16 * (t % 2) + 16])
        steps = [lambda: ts(T.nt[:, :], src, MAGIC, MAGIC, A.add, A.subtract, allown + ["turn"], ["nt"])]
        for x in range(8):
            steps.append(lambda x=x: ts(plane(T.nx, x), T.nt[:, :], T.rp[:, 16 * x + 15:16 * x + 16], 0.5, A.mult, A.mult, ["nt", "rp"], ["nx%d" % x]))

        def turn():
            for e1 in range(16):
                mm(SELF, e1, E, T.nx[:, e1:8 * E:16], T.k16[:, t:t + 16], True, True, ["k16"] + ["nx%d" % x for x in range(8)], 16)
        return steps + [turn, lambda: ts(T.off[:, :], ps(SELF, 0, E), 2048.0, None, A.add, None, ["ps" + SELF], ["off"], [SELF])]

    def prepare(t):
        par = t % 2
        mine = [owntok(par, 0), owntok(par, 1)]
        ts(T.n16[:, :], own(par), MAGIC, MAGIC, A.add, A.subtract, mine, ["n16"])
        mm(DELTA, 0, E, T.id32[:, :], own(par), True, False, ["id32"] + mine)
        mm(DELTA, 0, E, T.idh[:, :], T.n16[:, :], False, True, ["idh", "n16"])
        for i in range(4):
            bias = 199.5 if i == 0 else 191.5 * 2 ** i + 8
            act(plane(T.qm, i), ps(DELTA, 0, E), F.Identity, bias, 1.0, ["ps" + DELTA], ["qm%d" % i], [DELTA])
        act(T.ma[:, :], ps(DELTA, 0, E), F.Identity, 7.5, 1.0, ["ps" + DELTA], ["ma"], [DELTA])
        for h, b in enumerate(MINE):
            mm(b, 0, 2 * E, idb(2.0), plane(T.qc, 2 * h, 2), True, False, ["qc%d" % (2 * h), "qc%d" % (2 * h + 1)])
            mm(b, 0, 2 * E, idb(2.0), plane(T.qm, 2 * h, 2), False, False, ["qm%d" % (2 * h), "qm%d" % (2 * h + 1)])
            mm(b, 0, 2 * E, idb(-2.0), plane(T.qm, 2 * h + 1, 2), False, True, ["qm%d" % (2 * h + 1), "qm%d" % (2 * h + 2)])

    op("y", lambda: g.sync.dma_start(T.kin_i[:, :], T.kin[:, :]).then_inc(T.sem.loaded, 16), (), ["kin"], (), ("loaded", 16))
    op("g", lambda: g.iota(T.small[:, 0:32], [[1, 2], [2, 16]], 0, 32), (), ["small0"])
    op("g", lambda: g.iota(T.small[:, 32:64], [[-1, 32]], 32, 1), (), ["small1"])
    ms(T.one[:, :], 1.0, ["one"])
    ms(T.comb[:, :], 0.0, ["comb"])
    ms(T.lraw[:, :], math.log(2.0), ["lraw"])
    ms(T.comb[:, 15:144:16], 2.0, ["comb"])
    asel(T.id32[:, :], [[-1, 128]], A.is_equal, 0.0, 0, 1, "id32", T.one[:, :], "one")
    asel(T.rp[:, :], [[-1, 144]], A.is_ge, 0.0, 15, 1, "rp", T.comb[:, :], "comb")
    asel(T.rp[:, :], [[1, 144]], A.is_ge, 0.0, 0, -1, "rp")
    ms(T.ones[:, :], 1.0, ["ones"])
    ms(plane(T.qm, 4), 3072.0, ["qm4"])
    for j in range(4):
        ms(plane(T.qc, j), 192.0 * 2 ** j, ["qc%d" % j])
        ms(T.wm[32 * j:32 * (j + 1), :], 2.0 ** j / 32, ["wm%d" % j])
    ts(T.small[:, 64:96], T.small[:, 0:32], P - 1, None, A.bitwise_and, None, ["small0"], ["small2"])
    ts(T.small[:, 96:128], T.small[:, 32:64], 15, None, A.bitwise_and, None, ["small1"], ["small3"])
    cp(T.turn[:, :], T.small[:, 64:96], ["small2"], ["turn"])
    ts(T.k16[:, :], T.small[:, 96:128], 0.0, 1 / 16, A.is_equal, A.mult, ["small3"], ["k16"])
    cp(T.msg0[:, :], T.kin_i[:, :], ["kin"], ["msg0"])
    send(0, ["msg0"])
    op("g", lambda: g.iota(T.a32[:, :], [[16, P]], 16 * (P * r - 2048), 0, allow_small_or_imprecise_dtypes=True), (), ["a32"])
    asel(T.lraw[:, :], [[1, 128]], A.is_gt, -math.log(32.0), 0, -1, "lraw")
    asel(T.lraw[:, :], [[1, 128]], A.not_equal, -200.0, 0, -1, "lraw")
    asel(T.lraw[:, :], [[-16, 8], [0, 16]], A.is_ge, -200.0, 0, 1, "lraw")
    asel(T.lraw[:, :], [[16, 8], [0, 16]], A.is_ge, -200.0, 15, -1, "lraw")
    ts(T.tab[:, r * P:(r + 1) * P], T.msg0[:, :], -SHIFT, None, A.add, None, ["msg0"], allown)
    ts(T.idh[:, :], T.id32[:, :], -1.0, None, A.mult, None, ["id32"], ["idh"])
    for i, x in enumerate(IDB):
        ts(T.idb[:, 128 * i:128 * (i + 1)], T.id32[:, :], x, None, A.mult, None, ["id32"], ["idb%d" % i])
    op("p", None, ["idb%d" % i for i in range(len(IDB))])
    for step in offsets(0):
        step()
    prepare(0)
    act(T.tri[:, :], T.lraw[:, :], F.Exp, 0.0, 1.0, ["lraw"], ["tri"])
    for t in range(RO):
        q0 = 17 * t + 3
        ts(T.sel[:, 128 * t:128 * (t + 1)], T.one[:, :], T.id32[:, q0:q0 + 1], None, A.mult, None, ["one", "id32"], ["sel%d" % t])
    ts(T.vt[:, :], T.id32[:, :], -1.0, 2.0, A.mult, A.add, ["id32"], ["vt"])
    ts(T.vz[:, :], T.id32[:, :], 2.0, -4.0, A.mult, A.add, ["id32"], ["vz"])
    ts(T.vk[:, :], T.id32[:, :], 0.5, -1 / 256, A.mult, A.add, ["id32"], ["vk"])
    for s in senders:
        take(0, s)
        if s == senders[1]:
            cp(T.a16[:, :], T.a32[:, :], ["a32"], ["a16"])

    for t in range(RO):
        par = t % 2
        last = t == RO - 1
        sel, seltok = T.sel[:, 128 * t:128 * (t + 1)], "sel%d" % t

        def gather(e, lo, hi):
            src, out = T.tab[:, :].indirect(T.off[:, 8 * lo:8 * hi]), T.gat[:, H * lo:H * hi]
            toks = ["gat%d" % i for i in range(lo, hi)]
            if e == "v":
                cp(out, src, alltab + ["off"], toks)
            else:
                act(out, src, F.Identity, 0.0, 1.0, alltab + ["off"], toks)

        def name():
            ts(T.gb[:, :], plane(T.gat, 0), MAGIC, MAGIC, A.add, A.subtract, ["gat0", "gat1"], ["gb"])
            for i in range(2):
                mm(NAME, i * E, (i + 1) * E, sel, T.gb[:, :], True, True, [seltok, "gb"])
            mm(CODE, 0, E, idb(-1.0), T.ones[:, :], True, False, ["ones"])

        def sub(k, n):
            tt(plane(T.dif, k, n), plane(T.gat, k, n), ps(NAME, 0, n * E), A.subtract,
               ["gat%d" % i for i in range(2 * k, 2 * (k + n))] + ["ps" + NAME], ["dif%d" % i for i in range(k, k + n)], [NAME])

        def clamp(k, n):
            toks = ["dif%d" % i for i in range(k, k + n)]
            ts(plane(T.dif, k, n), plane(T.dif, k, n), -8.0, 8.0, A.max, A.min, toks, toks)
            for i in range(k, k + n):
                row = (t + i) % 16
                mm(CODE, 0, E, T.rp[:, 15 - row:143 - row], plane(T.dif, i), False, i == 15, ["dif%d" % i, "rp"])

        def half(buf, c, j=0):
            return buf[:, j * E + c * H:j * E + (c + 1) * H]

        def named(bank, lo, other, tok, sp=True):
            mm(bank, lo, lo + E, sel, T.gb[:, :], True, False, [seltok, "gb"])
            mm(bank, lo, lo + E, T.idh[:, :], other, False, sp, ["idh", tok])

        def selves():
            named(SELF, 0, T.n16[:, :], "n16")
            named(SELF, E, T.a16[:, par:P:2], "a16")

        def not_own():
            ts(plane(T.no, 0), ps(SELF, 0, E), 0.0, None, A.not_equal, None, ["ps" + SELF], ["no"], [SELF])

        def not_skipped():
            act(plane(T.sg, 0), ps(SELF, E, 2 * E), F.Sign, 0.0, 1.0, ["ps" + SELF], ["sg"], [SELF])
            act(plane(T.no, 1), plane(T.sg, 0), F.Abs, 0.0, 1.0, ["sg"], ["noskip"])

        def code(c):
            tt(half(T.pi, c), ps(CODE, c * H, (c + 1) * H), half(T.no, c), A.mult, ["ps" + CODE, "no"], ["pi%d" % c], [CODE])

        def bit(j, c=None):
            out, src = (plane(T.uu, j), T.pi[:, :]) if c is None else (half(T.uu, c, j), half(T.pi, c))
            cs = [0, 1] if c is None else [c]
            ts(out, src, 1 + (2 << j), None, A.bitwise_and, None, ["pi%d" % x for x in cs], ["u%d_%d" % (x, j) for x in cs])

        def speaks(j):
            ts(T.tes[:, :], plane(T.uu, j), (2 << j) + 0.5, None, A.is_lt, None, ["u0_%d" % j, "u1_%d" % j], ["tes"])

        def same(j):
            b = MINE[j // 2]
            tt(plane(T.zz, j), plane(T.uu, j), ps(b, j % 2 * E, (j % 2 + 1) * E), A.is_equal,
               ["u0_%d" % j, "u1_%d" % j, "ps" + b], ["z%d" % j], [b])

        def vote(j):
            mm(VOTE[j], 0, E, T.vt[:, :], T.tes[:, :], True, False, ["vt", "tes"])

        def vote_same(j):
            mm(VOTE[j], 0, E, T.vz[:, :], plane(T.zz, j), False, True, ["vz", "z%d" % j])

        def against(j):
            act(plane(T.gg, j), ps(VOTE[j], 0, E), F.Abs, -1.0, 1.0, ["ps" + VOTE[j]], ["g%d" % j], [VOTE[j]])

        def key_begin():
            mm(KEY, 0, E, idb(-9.0), plane(T.no, 0), True, False, ["no"])
            mm(KEY, 0, E, idb(60.0), plane(T.no, 1), False, False, ["noskip"])

        def key_silent():
            mm(KEY, 0, E, idb(40.0), T.tes[:, :], False, False, ["tes"])

        def key(j):
            mm(KEY, 0, E, T.vk[:, :], plane(T.gg, j), False, j == 3, ["vk", "g%d" % j])

        def elected(j):
            b = VOTE[j]
            tt(T.om[32 * j:32 * (j + 1), :], T["ps" + b][32 * j:32 * (j + 1), 0:E], T.zz[32 * j:32 * (j + 1), j * E:(j + 1) * E],
               A.is_gt, ["ps" + b, "z%d" % j], ["om%d" % j], [b])

        def change_begin():
            named(DELTA, 0, T.n16[:, :], "n16", False)
            mm(DELTA, 0, E, idb(-1.0), T.ma[:, :], False, False, ["ma"])

        def change():
            mm(DELTA, 0, E, T.wm[:, :], T.om[:, :], False, True, ["wm%d" % j for j in range(4)] + ["om%d" % j for j in range(4)])

        def power():
            act(T.xx[:, :], ps(KEY, 0, E), F.Exp, -91.0 * LN64, LN64, ["ps" + KEY], ["xx"], [KEY])

        def rivals():
            mm(RIVAL, 0, E, T.tri[:, :], T.xx[:, :], True, True, ["tri", "xx"])

        def first(c):
            tt(half(T.win, c), ps(RIVAL, c * H, (c + 1) * H), half(T.xx, c), A.is_lt, ["ps" + RIVAL, "xx"], ["win%d" % c], [RIVAL])

        def apply(c):
            tt(ps(DELTA, E + c * H, E + (c + 1) * H), ps(DELTA, c * H, (c + 1) * H), half(T.win, c), A.mult,
               ["ps" + DELTA, "win%d" % c], ["tt%d" % c], [DELTA])

        def update(c):
            o = own(par, c * H, (c + 1) * H)
            tt(o, ps(DELTA, E + c * H, E + (c + 1) * H), o, A.add, ["tt%d" % c, owntok(par, c)], [owntok(par, c)], [DELTA])

        def pack(c):
            lo, hi = c * H, (c + 1) * H
            out = T.yo[:, 2 * lo + par:2 * hi:2] if last else T["msg%d" % (t + 1)][:, lo:hi]
            ts(out, own(par, lo, hi), SHIFT, None, A.add, None, [owntok(par, c)], ["new%d" % c])

        gather("v", *BY_VECTOR[0])
        gather("v", *BY_VECTOR[1])
        name()
        gather("v", *BY_VECTOR[2])
        for lo, hi in BY_SCALAR:
            gather("s", lo, hi)
        selves(); change_begin(); sub(0, 2)
        for k in range(2, 14, 2):
            sub(k, 2); clamp(k - 2, 2)
        sub(14, 1); clamp(12, 2); sub(15, 1); clamp(14, 1); clamp(15, 1)
        nxt = offsets(t + 1) if not last else [lambda: None] * 10
        not_own(); not_skipped()
        code(0); code(1); key_begin(); bit(0, 0); bit(0, 1); bit(1); speaks(0); same(0); vote(0); vote_same(0); against(0); vote(1); bit(2)
        same(1); vote_same(1); against(1); vote(2); bit(3); same(2); vote_same(2); against(2); vote(3); key_silent()
        same(3); vote_same(3); against(3); key(0); key(1); key(2); key(3); power(); rivals()
        elected(0); elected(1); elected(2); elected(3); change(); nxt[0]()
        first(0); first(1); apply(0); apply(1); update(0); update(1); pack(0); pack(1)
        if last:
            act(T.yo[:, 1 - par:P:2], own(1 - par), F.Identity, SHIFT, 1.0, [owntok(1 - par, 0), owntok(1 - par, 1)], ["kept"])
            op("y", lambda: g.sync.dma_start(T.yk[:, :], T.yo[:, :]).then_inc(T.sem.stored, 16),
               ["new0", "new1", "kept"], ["yk1"], (), ("stored", 16))
        else:
            send(t + 1, ["new0", "new1"])
            for step in nxt[1:-1]:
                step()
            prepare(t + 1)
            for s in senders:
                take(t + 1, s)
                if s == senders[0]:
                    nxt[-1]()
    op("y", None, ["yk1"], ())
    op("g", None, ["out%d" % (RO - 1)], ())
    emit(g, T, ops)
